import numpy as np
import ml_dtypes


def mxq(x, axis, fmt="e4m3"):
    dtype, down = {"e4m3": (ml_dtypes.float8_e4m3fn, 7), "e5m2": (ml_dtypes.float8_e5m2, 14)}[fmt]
    v = np.moveaxis(np.asarray(x, np.float32).astype(ml_dtypes.bfloat16).astype(np.float64), axis, -1)
    blocks = v.reshape(v.shape[:-1] + (-1, 32))
    amax = np.abs(blocks).max(-1, keepdims=True)
    byte = np.maximum(np.where(amax > 0, np.frexp(amax)[1] - 1 + 127, 0) - down, 1)
    scale = np.exp2(byte - 127.0)
    codes = (blocks / scale).astype(np.float32).astype(dtype).astype(np.float64)
    return np.moveaxis((codes * scale).reshape(v.shape), -1, axis)


WIDE = False


def mx_kscale(k):
    if not WIDE:
        return np.ones(k)
    levels = np.array([10, -10, 5, -5, 0])
    if k % 512:
        return np.exp2(np.random.permutation(np.resize(levels, k // 32))).repeat(32)
    a = np.empty((k // 512, 16))
    for p in range(k // 512):
        a[p, :8] = np.random.permutation(np.resize(levels, 8))
        for g in range(8):
            far = levels[np.abs(levels - a[p, g]) >= 10]
            a[p, g + 8] = far[np.random.randint(len(far))]
    return np.exp2(a.ravel()).repeat(32)


def f64(x):
    return np.asarray(x).astype(np.float64)


def striped(idx):
    return np.tile(idx.reshape(-1, 16).T, (8, 1)).astype(np.uint16)


def unstriped(offs):
    return offs[:16].T.reshape(-1).astype(np.int64)


def relu(v):
    return np.maximum(v, 0.0)


K, T, D, S, V, N = 512, 2048, 2, 1024, 512, 256
P = 2 ** 7


def setup_inputs():
    n = np.random.standard_normal
    s = mx_kscale(K)[:, None]
    return {
        "xT": (n((K, T)) * s / np.sqrt(D)).astype(ml_dtypes.bfloat16).astype(np.float32),
        "w": (n((K, N)) / np.sqrt(K) / s).astype(np.float32),
        "b": (0.3 * n((N, 1))).astype(np.float32),
        "gate": np.tile(np.random.uniform(0.5, 1.5, (D, 1, V)), (1, P, 1)).astype(ml_dtypes.bfloat16).astype(np.float32),
        "offs": striped(np.concatenate([np.random.permutation(T)[:V] for _ in range(D)])),
    }


def reference(xT, w, b, gate, offs):
    idx = unstriped(offs)
    x = sum(f64(gate)[d, :1] * f64(xT)[:, idx[d * V:(d + 1) * V]] for d in range(D))
    return relu((mxq(f64(w), 0, "e4m3").T @ mxq(x, 0, "e4m3")) + f64(b))

@@ -1,0 +1,137 @@
+from contextlib import ExitStack
+
+import concourse.mybir as mybir
+from concourse.masks import make_identity
+
+K, T, D, V, N = 512, 2048, 2, 512, 256
+FLOPS = 2 * K * N * V
+
+F32 = mybir.dt.float32
+BF16 = mybir.dt.bfloat16
+U32 = mybir.dt.uint32
+U16 = mybir.dt.uint16
+U8 = mybir.dt.uint8
+FP8X4 = mybir.dt.float8_e4m3fn_x4
+ALU = mybir.AluOpType
+ACT = mybir.ActivationFunctionType
+
+P = 128
+PACK = 4
+CHUNKS = ((0, 256), (256, 128), (384, 128))
+
+
+def tile_picked_bag_lin_relu_sub_l_kernel(tc, xT, w, b, gate, offs, out):
+    nc = tc.nc
+    with ExitStack() as ctx:
+        keep = ctx.enter_context(tc.tile_pool(name="keep", bufs=1))
+        psum = ctx.enter_context(tc.psum_pool(name="psum", bufs=1))
+
+        offsets = keep.tile([P, D * V // 16], U16, name="offsets")
+        planes = [keep.tile([P, T], F32, name="plane%d" % t) for t in range(PACK)]
+        gate_col = keep.tile([P, D, PACK], F32, name="gate_col")
+        gates = keep.tile([P, D * V], F32, name="gates")
+        w_raw = keep.tile([P, PACK, N], F32, name="w_raw")
+        bias = keep.tile([P, N // P], F32, name="bias")
+        ident = keep.tile([P, P], F32, name="ident")
+        prods = keep.tile([P, PACK, D * V], F32, name="prods")
+        x_bf = keep.tile([P, V * PACK], BF16, name="x_bf", align_bytes=64)
+        w_bf = keep.tile([P, N * PACK], BF16, name="w_bf", align_bytes=64)
+        x_codes = keep.tile([P, V], U32, name="x_codes", align_bytes=64)
+        x_scales = keep.tile([P, V], U8, name="x_scales", align_bytes=64)
+        w_codes = keep.tile([P, N], U32, name="w_codes", align_bytes=64)
+        w_scales = keep.tile([P, N], U8, name="w_scales", align_bytes=64)
+        result = keep.tile([P, N // P, V], F32, name="result")
+
+        x_rows = xT.rearrange("(p t) c -> p t c", t=PACK)
+        nc.scalar.dma_start(out=gate_col[:], in_=gate[:, 0, :].rearrange("d (p j) -> p d j", j=PACK))
+        nc.sync.dma_start(out=planes[0][:], in_=x_rows[:, 0, :])
+        nc.sync.dma_start(offsets[:], offs)
+        for t in range(1, PACK):
+            nc.sync.dma_start(out=planes[t][:], in_=x_rows[:, t, :])
+        nc.sync.dma_start(out=w_raw[:], in_=w.rearrange("(p t) c -> p t c", t=PACK))
+        with nc.allow_non_contiguous_dma(reason="one bias value to a partition"):
+            nc.sync.dma_start(out=bias[:], in_=b.rearrange("(c p) o -> p (c o)", p=P))
+
+        make_identity(nc, ident[:])
+        for d in range(D):
+            spread = psum.tile([P, PACK, P], F32, name="spread%d" % d)
+            for j in range(PACK):
+                nc.tensor.transpose(spread[:, j, :], gate_col[:, d, j : j + 1].to_broadcast([P, P]), ident[:])
+            dst = gates[:, d * V : (d + 1) * V].rearrange("m (p j) -> m p j", j=PACK)
+            src = spread[:].rearrange("m j p -> m p j")
+            if d == 0:
+                nc.vector.tensor_copy(out=dst, in_=src)
+            else:
+                nc.scalar.activation(out=dst, in_=src, func=ACT.Copy)
+
+        def gather(t, e0, n):
+            nc.vector.tensor_tensor(
+                prods[:, t, e0 : e0 + n],
+                planes[t][:].indirect(offsets[:, e0 // 16 : (e0 + n) // 16]),
+                gates[:, e0 : e0 + n],
+                ALU.mult,
+            )
+
+        def add(c):
+            v0, n = CHUNKS[c]
+            nc.vector.tensor_tensor(
+                x_bf[:, v0 * PACK : (v0 + n) * PACK].rearrange("p (c i t) -> p c t i", i=2, t=PACK),
+                prods[:, :, v0 : v0 + n].rearrange("p t (c i) -> p c t i", i=2),
+                prods[:, :, V + v0 : V + v0 + n].rearrange("p t (c i) -> p c t i", i=2),
+                ALU.add,
+            )
+
+        def finish(c):
+            v0, n = CHUNKS[c]
+            cols = slice(v0, v0 + n)
+            nc.vector.quantize_mx(
+                out=x_codes[:, cols].bitcast(FP8X4),
+                scales=x_scales[:, cols],
+                in_=x_bf[:, v0 * PACK : (v0 + n) * PACK],
+            )
+            last = c == len(CHUNKS) - 1
+            for m in range(N // P):
+                acc = psum.tile([P, n], F32, name="acc%d_%d" % (c, m))
+                nc.tensor.matmul_mx(
+                    out=acc[:],
+                    lhsT=w_codes[:, m * P : (m + 1) * P].bitcast(FP8X4),
+                    lhsT_scale=w_scales[:, m * P : (m + 1) * P],
+                    rhs=x_codes[:, cols].bitcast(FP8X4),
+                    rhs_scale=x_scales[:, cols],
+                    start=True,
+                    stop=True,
+                )
+                if last and m == 1:
+                    nc.vector.tensor_scalar(result[:, m, cols], acc[:], bias[:, m : m + 1], 0.0, ALU.add, ALU.max)
+                    nc.sync.dma_start(out=out[m * P : (m + 1) * P, cols], in_=result[:, m, cols])
+                else:
+                    nc.scalar.activation(out=result[:, m, cols], in_=acc[:], func=ACT.Relu, bias=bias[:, m : m + 1])
+                    if last:
+                        nc.scalar.dma_start(out=out[m * P : (m + 1) * P, cols], in_=result[:, m, cols])
+            if not last:
+                nc.sync.dma_start(out=out.rearrange("(m p) v -> p m v", p=P)[:, :, cols], in_=result[:, :, cols])
+
+        gather(0, 0, V)
+        gather(0, V, V)
+        gather(1, 0, D * V)
+        gather(2, 0, D * V)
+
+        nc.scalar.activation(
+            out=w_bf[:].rearrange("p (c i t) -> p c t i", i=4, t=PACK),
+            in_=w_raw[:].rearrange("p t (c i) -> p c t i", i=4),
+            func=ACT.Copy,
+        )
+
+        gather(3, 0, 256)
+        gather(3, V, 256)
+        gather(3, 256, 128)
+        add(0)
+        gather(3, V + 256, 128)
+        nc.vector.quantize_mx(out=w_codes[:].bitcast(FP8X4), scales=w_scales[:], in_=w_bf[:])
+        finish(0)
+        gather(3, 384, 128)
+        add(1)
+        gather(3, V + 384, 128)
+        finish(1)
+        add(2)
+        finish(2)

@@ -35,15 +35,16 @@ def tile_picked_bag_lin_relu_sub_l_kernel(tc, xT, w, b, gate, offs, out):
         ident = keep.tile([P, P], F32, name="ident")
         prods = keep.tile([P, PACK, D * V], F32, name="prods")
         x_bf = keep.tile([P, V * PACK], BF16, name="x_bf", align_bytes=64)
-        w_bf = keep.tile([P, N * PACK], BF16, name="w_bf", align_bytes=64)
         x_codes = keep.tile([P, V], U32, name="x_codes", align_bytes=64)
         x_scales = keep.tile([P, V], U8, name="x_scales", align_bytes=64)
         w_codes = keep.tile([P, N], U32, name="w_codes", align_bytes=64)
         w_scales = keep.tile([P, N], U8, name="w_scales", align_bytes=64)
+        pairs = keep.tile([P, 2, V * 2], BF16, name="pairs", align_bytes=64)
+        turned = keep.tile([P, V // P, P * 2], BF16, name="turned", tag="staging", align_bytes=64)
         result = keep.tile([P, N // P, V], F32, name="result")
 
         x_rows = xT.rearrange("(p t) c -> p t c", t=PACK)
-        nc.scalar.dma_start(out=gate_col[:], in_=gate[:, 0, :].rearrange("d (p j) -> p d j", j=PACK))
+        nc.sync.dma_start(out=gate_col[:], in_=gate[:, 0, :].rearrange("d (p j) -> p d j", j=PACK))
         nc.sync.dma_start(out=planes[0][:], in_=x_rows[:, 0, :])
         nc.sync.dma_start(offsets[:], offs)
         for t in range(1, PACK):
@@ -54,7 +55,7 @@ def tile_picked_bag_lin_relu_sub_l_kernel(tc, xT, w, b, gate, offs, out):
 
         make_identity(nc, ident[:])
         for d in range(D):
-            spread = psum.tile([P, PACK, P], F32, name="spread%d" % d)
+            spread = psum.tile([P, PACK, P], F32, name="spread", tag="bank%d" % d)
             for j in range(PACK):
                 nc.tensor.transpose(spread[:, j, :], gate_col[:, d, j : j + 1].to_broadcast([P, P]), ident[:])
             dst = gates[:, d * V : (d + 1) * V].rearrange("m (p j) -> m p j", j=PACK)
@@ -75,11 +76,41 @@ def tile_picked_bag_lin_relu_sub_l_kernel(tc, xT, w, b, gate, offs, out):
         def add(c):
             v0, n = CHUNKS[c]
             nc.vector.tensor_tensor(
-                x_bf[:, v0 * PACK : (v0 + n) * PACK].rearrange("p (c i t) -> p c t i", i=2, t=PACK),
-                prods[:, :, v0 : v0 + n].rearrange("p t (c i) -> p c t i", i=2),
-                prods[:, :, V + v0 : V + v0 + n].rearrange("p t (c i) -> p c t i", i=2),
+                pairs[:, 1, v0 * 2 : (v0 + n) * 2].rearrange("p (c i e) -> p c e i", i=4, e=2),
+                prods[:, 2:4, v0 : v0 + n].rearrange("p e (c i) -> p c e i", i=4),
+                prods[:, 2:4, V + v0 : V + v0 + n].rearrange("p e (c i) -> p c e i", i=4),
                 ALU.add,
             )
+            nc.scalar.copy(
+                out=x_bf[:, v0 * PACK : (v0 + n) * PACK].bitcast(F32).rearrange("p (v u) -> p v u", u=2),
+                in_=pairs[:].bitcast(F32)[:, :, v0 : v0 + n].rearrange("p u v -> p v u"),
+            )
+
+        sums = [psum.tile([P, 2, 2, P], F32, name="sums", tag="bank%d" % (2 + h)) for h in range(2)]
+
+        def sum_turned(e):
+            for j in range(V // P):
+                for d in range(D):
+                    nc.tensor.matmul(
+                        sums[j // 2][:, j % 2, e, :],
+                        prods[:, e, d * V + j * P : d * V + (j + 1) * P],
+                        ident[:],
+                        start=(d == 0),
+                        stop=(d == D - 1),
+                        is_transpose=True,
+                    )
+
+        def turn_back():
+            words = psum.tile([P, V], F32, name="words", tag="bank4")
+            for h in range(2):
+                nc.scalar.activation(
+                    out=turned[:, 2 * h : 2 * h + 2, :].rearrange("v j (p e) -> v j p e", e=2),
+                    in_=sums[h][:].rearrange("v j e p -> v j p e"),
+                    func=ACT.Copy,
+                )
+                for j in range(2 * h, 2 * h + 2):
+                    nc.tensor.transpose(words[:, j * P : (j + 1) * P], turned[:, j, :].bitcast(F32), ident[:])
+            nc.scalar.copy(out=pairs[:, 0, :].bitcast(F32), in_=words[:])
 
         def finish(c):
             v0, n = CHUNKS[c]
@@ -91,7 +122,7 @@ def tile_picked_bag_lin_relu_sub_l_kernel(tc, xT, w, b, gate, offs, out):
             )
             last = c == len(CHUNKS) - 1
             for m in range(N // P):
-                acc = psum.tile([P, n], F32, name="acc%d_%d" % (c, m))
+                acc = psum.tile([P, n], F32, name="acc", tag="bank%d" % ((5 + 2 * c + m) % 8))
                 nc.tensor.matmul_mx(
                     out=acc[:],
                     lhsT=w_codes[:, m * P : (m + 1) * P].bitcast(FP8X4),
@@ -113,9 +144,13 @@ def tile_picked_bag_lin_relu_sub_l_kernel(tc, xT, w, b, gate, offs, out):
 
         gather(0, 0, V)
         gather(0, V, V)
+        sum_turned(0)
         gather(1, 0, D * V)
+        sum_turned(1)
         gather(2, 0, D * V)
+        turn_back()
 
+        w_bf = keep.tile([P, N * PACK], BF16, name="w_bf", tag="staging", align_bytes=64)
         nc.scalar.activation(
             out=w_bf[:].rearrange("p (c i t) -> p c t i", i=4, t=PACK),
             in_=w_raw[:].rearrange("p t (c i) -> p c t i", i=4),

@@ -17,7 +17,7 @@ ACT = mybir.ActivationFunctionType
 
 P = 128
 PACK = 4
-CHUNKS = ((0, 256), (256, 128), (384, 128))
+HALF = V // 2
 
 
 def tile_picked_bag_lin_relu_sub_l_kernel(tc, xT, w, b, gate, offs, out):
@@ -28,101 +28,130 @@ def tile_picked_bag_lin_relu_sub_l_kernel(tc, xT, w, b, gate, offs, out):
 
         offsets = keep.tile([P, D * V // 16], U16, name="offsets")
         planes = [keep.tile([P, T], F32, name="plane%d" % t) for t in range(PACK)]
-        gate_col = keep.tile([P, D, PACK], F32, name="gate_col")
+        gate_cols = keep.tile([P, D, 2 * PACK], F32, name="gate_cols")
+        gate_bf = keep.tile([P, D, PACK], BF16, name="gate_bf")
         gates = keep.tile([P, D * V], F32, name="gates")
-        w_raw = keep.tile([P, PACK, N], F32, name="w_raw")
+        w_raw = keep.tile([P, PACK, N], F32, name="w_raw", tag="w_slot", align_bytes=64)
         bias = keep.tile([P, N // P], F32, name="bias")
         ident = keep.tile([P, P], F32, name="ident")
-        prods = keep.tile([P, PACK, D * V], F32, name="prods")
-        x_bf = keep.tile([P, V * PACK], BF16, name="x_bf", align_bytes=64)
+        ident_bf = keep.tile([P, P], BF16, name="ident_bf")
+        early = keep.tile([P, 2, D * V], F32, name="early")
+        late = keep.tile([P, D, 2, V], F32, name="late")
+        pairs = keep.tile([P, 2 * (2 * V - P)], F32, name="pairs", align_bytes=64)
         x_codes = keep.tile([P, V], U32, name="x_codes", align_bytes=64)
         x_scales = keep.tile([P, V], U8, name="x_scales", align_bytes=64)
         w_codes = keep.tile([P, N], U32, name="w_codes", align_bytes=64)
         w_scales = keep.tile([P, N], U8, name="w_scales", align_bytes=64)
-        pairs = keep.tile([P, 2, V * 2], BF16, name="pairs", align_bytes=64)
         turned = keep.tile([P, V // P, P * 2], BF16, name="turned", tag="staging", align_bytes=64)
         result = keep.tile([P, N // P, V], F32, name="result")
 
         x_rows = xT.rearrange("(p t) c -> p t c", t=PACK)
-        nc.sync.dma_start(out=gate_col[:], in_=gate[:, 0, :].rearrange("d (p j) -> p d j", j=PACK))
-        nc.sync.dma_start(out=planes[0][:], in_=x_rows[:, 0, :])
+        nc.sync.dma_start(out=gate_cols[:, :, :PACK], in_=gate[:, 0, :].rearrange("d (p j) -> p d j", j=PACK))
+        nc.sync.dma_start(out=planes[2][:], in_=x_rows[:, 2, :])
         nc.sync.dma_start(offsets[:], offs)
-        for t in range(1, PACK):
+        for t in (3, 0, 1):
             nc.sync.dma_start(out=planes[t][:], in_=x_rows[:, t, :])
         nc.sync.dma_start(out=w_raw[:], in_=w.rearrange("(p t) c -> p t c", t=PACK))
         with nc.allow_non_contiguous_dma(reason="one bias value to a partition"):
             nc.sync.dma_start(out=bias[:], in_=b.rearrange("(c p) o -> p (c o)", p=P))
 
+        make_identity(nc, ident_bf[:])
         make_identity(nc, ident[:])
+        nc.vector.tensor_copy(out=gate_bf[:], in_=gate_cols[:, :, :PACK])
         for d in range(D):
-            spread = psum.tile([P, PACK, P], F32, name="spread", tag="bank%d" % d)
+            spread = psum.tile([P, PACK, P], BF16, name="spread", tag="bank%d" % d)
             for j in range(PACK):
-                nc.tensor.transpose(spread[:, j, :], gate_col[:, d, j : j + 1].to_broadcast([P, P]), ident[:])
-            dst = gates[:, d * V : (d + 1) * V].rearrange("m (p j) -> m p j", j=PACK)
-            src = spread[:].rearrange("m j p -> m p j")
-            if d == 0:
-                nc.vector.tensor_copy(out=dst, in_=src)
-            else:
-                nc.scalar.activation(out=dst, in_=src, func=ACT.Copy)
+                nc.tensor.transpose(spread[:, j, :], gate_bf[:, d, j : j + 1].to_broadcast([P, P]), ident_bf[:])
+            nc.vector.tensor_copy(
+                out=gates[:, d * V : (d + 1) * V].rearrange("m (p j) -> m p j", j=PACK),
+                in_=spread[:].rearrange("m j p -> m p j"),
+            )
 
-        def gather(t, e0, n):
+        sums = [psum.tile([P, 2, P], F32, name="sums", tag="bank%d" % (2 + j)) for j in range(V // P)]
+
+        def gather(dst, t, e0, n):
             nc.vector.tensor_tensor(
-                prods[:, t, e0 : e0 + n],
+                dst,
                 planes[t][:].indirect(offsets[:, e0 // 16 : (e0 + n) // 16]),
                 gates[:, e0 : e0 + n],
                 ALU.mult,
             )
 
-        def add(c):
-            v0, n = CHUNKS[c]
-            nc.vector.tensor_tensor(
-                pairs[:, 1, v0 * 2 : (v0 + n) * 2].rearrange("p (c i e) -> p c e i", i=4, e=2),
-                prods[:, 2:4, v0 : v0 + n].rearrange("p e (c i) -> p c e i", i=4),
-                prods[:, 2:4, V + v0 : V + v0 + n].rearrange("p e (c i) -> p c e i", i=4),
-                ALU.add,
-            )
-            nc.scalar.copy(
-                out=x_bf[:, v0 * PACK : (v0 + n) * PACK].bitcast(F32).rearrange("p (v u) -> p v u", u=2),
-                in_=pairs[:].bitcast(F32)[:, :, v0 : v0 + n].rearrange("p u v -> p v u"),
-            )
-
-        sums = [psum.tile([P, 2, 2, P], F32, name="sums", tag="bank%d" % (2 + h)) for h in range(2)]
+        def gather_last(d, v0, n):
+            gather(late[:, d, 1, v0 : v0 + n], 1, d * V + v0, n)
 
         def sum_turned(e):
             for j in range(V // P):
                 for d in range(D):
                     nc.tensor.matmul(
-                        sums[j // 2][:, j % 2, e, :],
-                        prods[:, e, d * V + j * P : d * V + (j + 1) * P],
+                        sums[j][:, e, :],
+                        early[:, e, d * V + j * P : d * V + (j + 1) * P],
                         ident[:],
                         start=(d == 0),
                         stop=(d == D - 1),
                         is_transpose=True,
                     )
 
-        def turn_back():
-            words = psum.tile([P, V], F32, name="words", tag="bank4")
-            for h in range(2):
-                nc.scalar.activation(
-                    out=turned[:, 2 * h : 2 * h + 2, :].rearrange("v j (p e) -> v j p e", e=2),
-                    in_=sums[h][:].rearrange("v j e p -> v j p e"),
-                    func=ACT.Copy,
-                )
-                for j in range(2 * h, 2 * h + 2):
-                    nc.tensor.transpose(words[:, j * P : (j + 1) * P], turned[:, j, :].bitcast(F32), ident[:])
-            nc.scalar.copy(out=pairs[:, 0, :].bitcast(F32), in_=words[:])
+        for d in range(D):
+            gather(early[:, 0, d * V : (d + 1) * V], 2, d * V, V)
+        sum_turned(0)
+        gather(early[:, 1, :], 3, 0, D * V)
+        sum_turned(1)
+        for d in range(D):
+            gather(late[:, d, 0, :], 0, d * V, V)
 
-        def finish(c):
-            v0, n = CHUNKS[c]
-            cols = slice(v0, v0 + n)
+        words = psum.tile([P, V], F32, name="words", tag="bank6")
+        for j in range(V // P):
+            nc.scalar.activation(
+                out=turned[:, j, :].rearrange("v (p e) -> v p e", e=2),
+                in_=sums[j][:].rearrange("v e p -> v p e"),
+                func=ACT.Copy,
+            )
+            nc.tensor.transpose(words[:, j * P : (j + 1) * P], turned[:, j, :].bitcast(F32), ident[:])
+        nc.scalar.copy(out=pairs[:, V : 2 * V], in_=words[:])
+
+        w_bf = keep.tile([P, N * PACK], BF16, name="w_bf", tag="staging", align_bytes=64)
+        nc.scalar.activation(
+            out=w_bf[:].rearrange("p (c i t) -> p c t i", i=4, t=PACK),
+            in_=w_raw[:].rearrange("p t (c i) -> p c t i", i=4),
+            func=ACT.Copy,
+        )
+        x_bf = keep.tile([P, V * PACK], BF16, name="x_bf", tag="w_slot", align_bytes=64)
+
+        def add(v0, n):
+            low = V - v0 - n
+            apart = 2 * v0 + n
+            nc.vector.tensor_tensor(
+                pairs[:, low : low + n].bitcast(BF16).rearrange("p (c i e) -> p c e i", i=4, e=2),
+                late[:, 0, :, v0 : v0 + n].rearrange("p e (c i) -> p c e i", i=4),
+                late[:, 1, :, v0 : v0 + n].rearrange("p e (c i) -> p c e i", i=4),
+                ALU.add,
+            )
+            nc.scalar.copy(
+                out=x_bf[:, v0 * PACK : (v0 + n) * PACK].bitcast(F32).rearrange("p (v u) -> p v u", u=2),
+                in_=pairs[:, low : low + 2 * apart].rearrange("p (u v) -> p v u", u=2)[:, :n, :],
+            )
+
+        gather_last(0, 0, HALF)
+        gather_last(1, 0, HALF)
+        gather_last(0, HALF, HALF)
+        add(0, HALF)
+        gather_last(1, HALF, P)
+        gather_last(1, HALF + P, P)
+        add(HALF, P)
+        add(HALF + P, P)
+        nc.vector.quantize_mx(out=w_codes[:].bitcast(FP8X4), scales=w_scales[:], in_=w_bf[:])
+        accs = []
+        for h in range(2):
+            cols = slice(h * HALF, (h + 1) * HALF)
             nc.vector.quantize_mx(
                 out=x_codes[:, cols].bitcast(FP8X4),
                 scales=x_scales[:, cols],
-                in_=x_bf[:, v0 * PACK : (v0 + n) * PACK],
+                in_=x_bf[:, h * HALF * PACK : (h + 1) * HALF * PACK],
             )
-            last = c == len(CHUNKS) - 1
             for m in range(N // P):
-                acc = psum.tile([P, n], F32, name="acc", tag="bank%d" % ((5 + 2 * c + m) % 8))
+                acc = psum.tile([P, HALF], F32, name="acc", tag="bank%d" % ((7 + 2 * h + m) % 8))
+                accs.append(acc)
                 nc.tensor.matmul_mx(
                     out=acc[:],
                     lhsT=w_codes[:, m * P : (m + 1) * P].bitcast(FP8X4),
@@ -132,41 +161,9 @@ def tile_picked_bag_lin_relu_sub_l_kernel(tc, xT, w, b, gate, offs, out):
                     start=True,
                     stop=True,
                 )
-                if last and m == 1:
-                    nc.vector.tensor_scalar(result[:, m, cols], acc[:], bias[:, m : m + 1], 0.0, ALU.add, ALU.max)
-                    nc.sync.dma_start(out=out[m * P : (m + 1) * P, cols], in_=result[:, m, cols])
-                else:
-                    nc.scalar.activation(out=result[:, m, cols], in_=acc[:], func=ACT.Relu, bias=bias[:, m : m + 1])
-                    if last:
-                        nc.scalar.dma_start(out=out[m * P : (m + 1) * P, cols], in_=result[:, m, cols])
-            if not last:
-                nc.sync.dma_start(out=out.rearrange("(m p) v -> p m v", p=P)[:, :, cols], in_=result[:, :, cols])
-
-        gather(0, 0, V)
-        gather(0, V, V)
-        sum_turned(0)
-        gather(1, 0, D * V)
-        sum_turned(1)
-        gather(2, 0, D * V)
-        turn_back()
-
-        w_bf = keep.tile([P, N * PACK], BF16, name="w_bf", tag="staging", align_bytes=64)
-        nc.scalar.activation(
-            out=w_bf[:].rearrange("p (c i t) -> p c t i", i=4, t=PACK),
-            in_=w_raw[:].rearrange("p t (c i) -> p c t i", i=4),
-            func=ACT.Copy,
-        )
-
-        gather(3, 0, 256)
-        gather(3, V, 256)
-        gather(3, 256, 128)
-        add(0)
-        gather(3, V + 256, 128)
-        nc.vector.quantize_mx(out=w_codes[:].bitcast(FP8X4), scales=w_scales[:], in_=w_bf[:])
-        finish(0)
-        gather(3, 384, 128)
-        add(1)
-        gather(3, V + 384, 128)
-        finish(1)
-        add(2)
-        finish(2)
+        for h in range(2):
+            cols = slice(h * HALF, (h + 1) * HALF)
+            nc.scalar.activation(out=result[:, 0, cols], in_=accs[2 * h][:], func=ACT.Relu, bias=bias[:, 0:1])
+            nc.scalar.dma_start(out=out[0:P, cols], in_=result[:, 0, cols])
+            nc.vector.tensor_scalar(result[:, 1, cols], accs[2 * h + 1][:], bias[:, 1:2], 0.0, ALU.add, ALU.max)
+            nc.sync.dma_start(out=out[P : 2 * P, cols], in_=result[:, 1, cols])

@@ -17,7 +17,10 @@ ACT = mybir.ActivationFunctionType
 
 P = 128
 PACK = 4
-HALF = V // 2
+HIGH_ORDER = (2, 3, 0, 1)
+X0_AT = D * V + 3 * P
+LAST_AT = {(2, 0): D * V, (2, 1): D * V + P, (3, 0): D * V + 2 * P, (3, 1): D * V + 5 * P}
+LATE_WORDS = 2 * (D * V + 5 * P) - (V + 3 * P)
 
 
 def tile_picked_bag_lin_relu_sub_l_kernel(tc, xT, w, b, gate, offs, out):
@@ -31,19 +34,22 @@ def tile_picked_bag_lin_relu_sub_l_kernel(tc, xT, w, b, gate, offs, out):
         gate_cols = keep.tile([P, D, 2 * PACK], F32, name="gate_cols")
         gate_bf = keep.tile([P, D, PACK], BF16, name="gate_bf")
         gates = keep.tile([P, D * V], F32, name="gates")
-        w_raw = keep.tile([P, PACK, N], F32, name="w_raw", tag="w_slot", align_bytes=64)
+        w_raw = keep.tile([P, PACK, N], F32, name="w_raw")
         bias = keep.tile([P, N // P], F32, name="bias")
         ident = keep.tile([P, P], F32, name="ident")
         ident_bf = keep.tile([P, P], BF16, name="ident_bf")
         early = keep.tile([P, 2, D * V], F32, name="early")
-        late = keep.tile([P, D, 2, V], F32, name="late")
-        pairs = keep.tile([P, 2 * (2 * V - P)], F32, name="pairs", align_bytes=64)
+        turned = keep.tile([P, V // P, P * 2], BF16, name="turned", tag="staging", align_bytes=64)
+        turned_late = keep.tile([P, 2, P * 2], BF16, name="turned_late", align_bytes=64)
+        last_pe = keep.tile([P, 2, D, P], F32, name="last_pe")
+        late = keep.tile([P, LATE_WORDS], F32, name="late", align_bytes=64)
+        x_bf1 = keep.tile([P, P * PACK], BF16, name="x_bf1", align_bytes=64)
+        x_bf23 = keep.tile([P, 2 * P * PACK], BF16, name="x_bf23", align_bytes=64)
         x_codes = keep.tile([P, V], U32, name="x_codes", align_bytes=64)
         x_scales = keep.tile([P, V], U8, name="x_scales", align_bytes=64)
         w_codes = keep.tile([P, N], U32, name="w_codes", align_bytes=64)
         w_scales = keep.tile([P, N], U8, name="w_scales", align_bytes=64)
-        turned = keep.tile([P, V // P, P * 2], BF16, name="turned", tag="staging", align_bytes=64)
-        result = keep.tile([P, N // P, V], F32, name="result")
+        result = keep.tile([P, V // P, N // P, P], F32, name="result")
 
         x_rows = xT.rearrange("(p t) c -> p t c", t=PACK)
         nc.sync.dma_start(out=gate_cols[:, :, :PACK], in_=gate[:, 0, :].rearrange("d (p j) -> p d j", j=PACK))
@@ -62,12 +68,14 @@ def tile_picked_bag_lin_relu_sub_l_kernel(tc, xT, w, b, gate, offs, out):
             spread = psum.tile([P, PACK, P], BF16, name="spread", tag="bank%d" % d)
             for j in range(PACK):
                 nc.tensor.transpose(spread[:, j, :], gate_bf[:, d, j : j + 1].to_broadcast([P, P]), ident_bf[:])
-            nc.vector.tensor_copy(
+            copy_out = nc.vector.tensor_copy if d == 0 else nc.scalar.copy
+            copy_out(
                 out=gates[:, d * V : (d + 1) * V].rearrange("m (p j) -> m p j", j=PACK),
                 in_=spread[:].rearrange("m j p -> m p j"),
             )
 
-        sums = [psum.tile([P, 2, P], F32, name="sums", tag="bank%d" % (2 + j)) for j in range(V // P)]
+        sums = [psum.tile([P, 4, P], F32, name="sums", tag="bank%d" % (2 + j)) for j in range(V // P)]
+        words = [psum.tile([P, 2, P], F32, name="words", tag="bank%d" % bank) for bank in (6, 7, 0)]
 
         def gather(dst, t, e0, n):
             nc.vector.tensor_tensor(
@@ -77,83 +85,100 @@ def tile_picked_bag_lin_relu_sub_l_kernel(tc, xT, w, b, gate, offs, out):
                 ALU.mult,
             )
 
-        def gather_last(d, v0, n):
-            gather(late[:, d, 1, v0 : v0 + n], 1, d * V + v0, n)
+        def sum_turned(dst, pieces):
+            for d in range(D):
+                nc.tensor.matmul(dst, pieces[d], ident[:], start=(d == 0), stop=(d == D - 1), is_transpose=True)
 
-        def sum_turned(e):
-            for j in range(V // P):
-                for d in range(D):
-                    nc.tensor.matmul(
-                        sums[j][:, e, :],
-                        early[:, e, d * V + j * P : d * V + (j + 1) * P],
-                        ident[:],
-                        start=(d == 0),
-                        stop=(d == D - 1),
-                        is_transpose=True,
-                    )
-
-        for d in range(D):
-            gather(early[:, 0, d * V : (d + 1) * V], 2, d * V, V)
-        sum_turned(0)
-        gather(early[:, 1, :], 3, 0, D * V)
-        sum_turned(1)
-        for d in range(D):
-            gather(late[:, d, 0, :], 0, d * V, V)
-
-        words = psum.tile([P, V], F32, name="words", tag="bank6")
-        for j in range(V // P):
+        def round_pairs(dst, src):
             nc.scalar.activation(
-                out=turned[:, j, :].rearrange("v (p e) -> v p e", e=2),
-                in_=sums[j][:].rearrange("v e p -> v p e"),
-                func=ACT.Copy,
+                out=dst.rearrange("v (p e) -> v p e", e=2), in_=src.rearrange("v e p -> v p e"), func=ACT.Copy
             )
-            nc.tensor.transpose(words[:, j * P : (j + 1) * P], turned[:, j, :].bitcast(F32), ident[:])
-        nc.scalar.copy(out=pairs[:, V : 2 * V], in_=words[:])
 
+        for e in range(2):
+            gather(early[:, e, :], 2 + e, 0, D * V)
+            for j in HIGH_ORDER:
+                sum_turned(sums[j][:, e, :], [early[:, e, d * V + j * P : d * V + (j + 1) * P] for d in range(D)])
+        gather(late[:, : D * V], 0, 0, D * V)
+
+        for j in HIGH_ORDER:
+            round_pairs(turned[:, j, :], sums[j][:, 0:2, :])
+            high = words[j][:, 1, :] if j < 2 else words[2][:, j - 2, :]
+            nc.tensor.transpose(high, turned[:, j, :].bitcast(F32), ident[:])
+        nc.scalar.copy(
+            out=x_bf23[:].bitcast(F32).rearrange("p (v u) -> p v u", u=2)[:, :, 1],
+            in_=words[2][:].rearrange("p j v -> p (j v)"),
+        )
+
+        for j in range(2):
+            sum_turned(sums[j][:, 2, :], [late[:, d * V + j * P : d * V + (j + 1) * P] for d in range(D)])
+
+        x_bf = [late[:, X0_AT : X0_AT + 2 * P].bitcast(BF16), x_bf1[:], x_bf23[:, : P * PACK], x_bf23[:, P * PACK :]]
         w_bf = keep.tile([P, N * PACK], BF16, name="w_bf", tag="staging", align_bytes=64)
+
+        def low_pairs(j):
+            sum_turned(sums[j][:, 3, :], [last_pe[:, j, d, :] for d in range(D)])
+            round_pairs(turned_late[:, j, :], sums[j][:, 2:4, :])
+            nc.tensor.transpose(words[j][:, 0, :], turned_late[:, j, :].bitcast(F32), ident[:])
+
+        def interleave(j):
+            nc.scalar.copy(
+                out=x_bf[j].bitcast(F32).rearrange("p (v u) -> p v u", u=2), in_=words[j][:].rearrange("p u v -> p v u")
+            )
+
+        def add(j):
+            def planes_0_1(d):
+                first = d * V + j * P
+                apart = LAST_AT[j, d] - first
+                both = late[:, first : first + 2 * apart].rearrange("p (e s) -> p e s", e=2)[:, :, :P]
+                return both.rearrange("p e (c i) -> p c e i", i=4)
+
+            nc.vector.tensor_tensor(
+                x_bf[j].rearrange("p (c i t) -> p c t i", i=4, t=PACK)[:, :, 0:2, :],
+                planes_0_1(0),
+                planes_0_1(1),
+                ALU.add,
+            )
+
+        def quantize(j):
+            nc.vector.quantize_mx(
+                out=x_codes[:, j * P : (j + 1) * P].bitcast(FP8X4), scales=x_scales[:, j * P : (j + 1) * P], in_=x_bf[j]
+            )
+
+        for j in range(2):
+            for d in range(D):
+                gather(last_pe[:, j, d, :], 1, d * V + j * P, P)
+        low_pairs(0)
         nc.scalar.activation(
             out=w_bf[:].rearrange("p (c i t) -> p c t i", i=4, t=PACK),
             in_=w_raw[:].rearrange("p t (c i) -> p c t i", i=4),
             func=ACT.Copy,
         )
-        x_bf = keep.tile([P, V * PACK], BF16, name="x_bf", tag="w_slot", align_bytes=64)
-
-        def add(v0, n):
-            low = V - v0 - n
-            apart = 2 * v0 + n
-            nc.vector.tensor_tensor(
-                pairs[:, low : low + n].bitcast(BF16).rearrange("p (c i e) -> p c e i", i=4, e=2),
-                late[:, 0, :, v0 : v0 + n].rearrange("p e (c i) -> p c e i", i=4),
-                late[:, 1, :, v0 : v0 + n].rearrange("p e (c i) -> p c e i", i=4),
-                ALU.add,
-            )
-            nc.scalar.copy(
-                out=x_bf[:, v0 * PACK : (v0 + n) * PACK].bitcast(F32).rearrange("p (v u) -> p v u", u=2),
-                in_=pairs[:, low : low + 2 * apart].rearrange("p (u v) -> p v u", u=2)[:, :n, :],
-            )
-
-        gather_last(0, 0, HALF)
-        gather_last(1, 0, HALF)
-        gather_last(0, HALF, HALF)
-        add(0, HALF)
-        gather_last(1, HALF, P)
-        gather_last(1, HALF + P, P)
-        add(HALF, P)
-        add(HALF + P, P)
+        low_pairs(1)
+        interleave(0)
+        interleave(1)
+        for j, d in ((2, 0), (2, 1), (3, 0)):
+            gather(late[:, LAST_AT[j, d] : LAST_AT[j, d] + P], 1, d * V + j * P, P)
+        add(2)
+        gather(late[:, LAST_AT[3, 1] : LAST_AT[3, 1] + P], 1, V + 3 * P, P)
+        quantize(2)
         nc.vector.quantize_mx(out=w_codes[:].bitcast(FP8X4), scales=w_scales[:], in_=w_bf[:])
-        accs = []
-        for h in range(2):
-            cols = slice(h * HALF, (h + 1) * HALF)
-            nc.vector.quantize_mx(
-                out=x_codes[:, cols].bitcast(FP8X4),
-                scales=x_scales[:, cols],
-                in_=x_bf[:, h * HALF * PACK : (h + 1) * HALF * PACK],
-            )
+        quantize(0)
+        add(3)
+        quantize(1)
+        quantize(3)
+
+        out_rows = out.rearrange("(m p) v -> p m v", p=P)
+        acc_banks = {2: (7, 7), 0: (6, 6), 1: (2, 3), 3: (4, 5)}
+        for j in (2, 0, 1, 3):
+            cols = slice(j * P, (j + 1) * P)
+            if acc_banks[j][0] == acc_banks[j][1]:
+                both = psum.tile([P, 2, P], F32, name="acc", tag="bank%d" % acc_banks[j][0])
+                accs = [both[:, m, :] for m in range(2)]
+            else:
+                accs = [psum.tile([P, P], F32, name="acc", tag="bank%d" % bank)[:] for bank in acc_banks[j]]
             for m in range(N // P):
-                acc = psum.tile([P, HALF], F32, name="acc", tag="bank%d" % ((7 + 2 * h + m) % 8))
-                accs.append(acc)
                 nc.tensor.matmul_mx(
-                    out=acc[:],
+                    out=accs[m],
                     lhsT=w_codes[:, m * P : (m + 1) * P].bitcast(FP8X4),
                     lhsT_scale=w_scales[:, m * P : (m + 1) * P],
                     rhs=x_codes[:, cols].bitcast(FP8X4),
@@ -161,9 +186,13 @@ def tile_picked_bag_lin_relu_sub_l_kernel(tc, xT, w, b, gate, offs, out):
                     start=True,
                     stop=True,
                 )
-        for h in range(2):
-            cols = slice(h * HALF, (h + 1) * HALF)
-            nc.scalar.activation(out=result[:, 0, cols], in_=accs[2 * h][:], func=ACT.Relu, bias=bias[:, 0:1])
-            nc.scalar.dma_start(out=out[0:P, cols], in_=result[:, 0, cols])
-            nc.vector.tensor_scalar(result[:, 1, cols], accs[2 * h + 1][:], bias[:, 1:2], 0.0, ALU.add, ALU.max)
-            nc.sync.dma_start(out=out[P : 2 * P, cols], in_=result[:, 1, cols])
+            nc.scalar.activation(out=result[:, j, 0, :], in_=accs[0], func=ACT.Relu, bias=bias[:, 0:1])
+            if j in (2, 0):
+                nc.scalar.activation(out=result[:, j, 1, :], in_=accs[1], func=ACT.Relu, bias=bias[:, 1:2])
+            else:
+                nc.vector.tensor_scalar(result[:, j, 1, :], accs[1], bias[:, 1:2], 0.0, ALU.add, ALU.max)
+            if j != 3:
+                nc.sync.dma_start(out=out_rows[:, :, cols], in_=result[:, j, :, :])
+            else:
+                nc.scalar.dma_start(out=out_rows[:, 0, cols], in_=result[:, j, 0, :])
+                nc.sync.dma_start(out=out_rows[:, 1, cols], in_=result[:, j, 1, :])

@@ -130,10 +130,10 @@ def tile_picked_bag_lin_relu_sub_l_kernel(tc, xT, w, b, gate, offs, out):
                 first = d * V + j * P
                 apart = LAST_AT[j, d] - first
                 both = late[:, first : first + 2 * apart].rearrange("p (e s) -> p e s", e=2)[:, :, :P]
-                return both.rearrange("p e (c i) -> p c e i", i=4)
+                return both.rearrange("p e (c i) -> p c e i", i=2)
 
             nc.vector.tensor_tensor(
-                x_bf[j].rearrange("p (c i t) -> p c t i", i=4, t=PACK)[:, :, 0:2, :],
+                x_bf[j].rearrange("p (c i t) -> p c t i", i=2, t=PACK)[:, :, 0:2, :],
                 planes_0_1(0),
                 planes_0_1(1),
                 ALU.add,

@@ -18,9 +18,8 @@ ACT = mybir.ActivationFunctionType
 P = 128
 PACK = 4
 HIGH_ORDER = (2, 3, 0, 1)
-X0_AT = D * V + 3 * P
-LAST_AT = {(2, 0): D * V, (2, 1): D * V + P, (3, 0): D * V + 2 * P, (3, 1): D * V + 5 * P}
-LATE_WORDS = 2 * (D * V + 5 * P) - (V + 3 * P)
+LAST_AT = {(2, 0): D * V, (3, 0): D * V + P, (2, 1): D * V + 2 * P, (3, 1): D * V + 3 * P}
+LATE_WORDS = 2 * D * V - P
 
 
 def tile_picked_bag_lin_relu_sub_l_kernel(tc, xT, w, b, gate, offs, out):
@@ -40,16 +39,16 @@ def tile_picked_bag_lin_relu_sub_l_kernel(tc, xT, w, b, gate, offs, out):
         ident_bf = keep.tile([P, P], BF16, name="ident_bf")
         early = keep.tile([P, 2, D * V], F32, name="early")
         turned = keep.tile([P, V // P, P * 2], BF16, name="turned", tag="staging", align_bytes=64)
-        turned_late = keep.tile([P, 2, P * 2], BF16, name="turned_late", align_bytes=64)
+        turned_late = keep.tile([P, 2, P * 2], BF16, name="turned_late", tag="low_slot", align_bytes=64)
+        x_bf0 = keep.tile([P, P * PACK], BF16, name="x_bf0", align_bytes=64)
         last_pe = keep.tile([P, 2, D, P], F32, name="last_pe")
         late = keep.tile([P, LATE_WORDS], F32, name="late", align_bytes=64)
         x_bf1 = keep.tile([P, P * PACK], BF16, name="x_bf1", align_bytes=64)
         x_bf23 = keep.tile([P, 2 * P * PACK], BF16, name="x_bf23", align_bytes=64)
         x_codes = keep.tile([P, V], U32, name="x_codes", align_bytes=64)
         x_scales = keep.tile([P, V], U8, name="x_scales", align_bytes=64)
-        w_codes = keep.tile([P, N], U32, name="w_codes", align_bytes=64)
         w_scales = keep.tile([P, N], U8, name="w_scales", align_bytes=64)
-        result = keep.tile([P, V // P, N // P, P], F32, name="result")
+        result = keep.tile([P, N // P, V], F32, name="result")
 
         x_rows = xT.rearrange("(p t) c -> p t c", t=PACK)
         nc.sync.dma_start(out=gate_cols[:, :, :PACK], in_=gate[:, 0, :].rearrange("d (p j) -> p d j", j=PACK))
@@ -105,14 +104,14 @@ def tile_picked_bag_lin_relu_sub_l_kernel(tc, xT, w, b, gate, offs, out):
             high = words[j][:, 1, :] if j < 2 else words[2][:, j - 2, :]
             nc.tensor.transpose(high, turned[:, j, :].bitcast(F32), ident[:])
         nc.scalar.copy(
-            out=x_bf23[:].bitcast(F32).rearrange("p (v u) -> p v u", u=2)[:, :, 1],
-            in_=words[2][:].rearrange("p j v -> p (j v)"),
+            out=x_bf23[:].bitcast(F32).rearrange("p (v u) -> p v u", u=2),
+            in_=words[2][:].rearrange("p j v -> p (j v)").unsqueeze(2).to_broadcast([P, 2 * P, 2]),
         )
 
         for j in range(2):
             sum_turned(sums[j][:, 2, :], [late[:, d * V + j * P : d * V + (j + 1) * P] for d in range(D)])
 
-        x_bf = [late[:, X0_AT : X0_AT + 2 * P].bitcast(BF16), x_bf1[:], x_bf23[:, : P * PACK], x_bf23[:, P * PACK :]]
+        x_bf = [x_bf0[:], x_bf1[:], x_bf23[:, : P * PACK], x_bf23[:, P * PACK :]]
         w_bf = keep.tile([P, N * PACK], BF16, name="w_bf", tag="staging", align_bytes=64)
 
         def low_pairs(j):
@@ -156,43 +155,48 @@ def tile_picked_bag_lin_relu_sub_l_kernel(tc, xT, w, b, gate, offs, out):
         low_pairs(1)
         interleave(0)
         interleave(1)
-        for j, d in ((2, 0), (2, 1), (3, 0)):
-            gather(late[:, LAST_AT[j, d] : LAST_AT[j, d] + P], 1, d * V + j * P, P)
+        gather(late[:, LAST_AT[2, 1] : LAST_AT[2, 1] + P], 1, V + 2 * P, P)
+        gather(late[:, LAST_AT[2, 0] : LAST_AT[2, 0] + 2 * P], 1, 2 * P, 2 * P)
         add(2)
         gather(late[:, LAST_AT[3, 1] : LAST_AT[3, 1] + P], 1, V + 3 * P, P)
         quantize(2)
-        nc.vector.quantize_mx(out=w_codes[:].bitcast(FP8X4), scales=w_scales[:], in_=w_bf[:])
-        quantize(0)
         add(3)
+        w_codes = keep.tile([P, N], U32, name="w_codes", tag="low_slot", align_bytes=64)
+        for m, j in ((0, 3), (1, 0)):
+            nc.vector.quantize_mx(
+                out=w_codes[:, m * P : (m + 1) * P].bitcast(FP8X4),
+                scales=w_scales[:, m * P : (m + 1) * P],
+                in_=w_bf[:, m * P * PACK : (m + 1) * P * PACK],
+            )
+            quantize(j)
         quantize(1)
-        quantize(3)
 
-        out_rows = out.rearrange("(m p) v -> p m v", p=P)
-        acc_banks = {2: (7, 7), 0: (6, 6), 1: (2, 3), 3: (4, 5)}
-        for j in (2, 0, 1, 3):
-            cols = slice(j * P, (j + 1) * P)
-            if acc_banks[j][0] == acc_banks[j][1]:
-                both = psum.tile([P, 2, P], F32, name="acc", tag="bank%d" % acc_banks[j][0])
-                accs = [both[:, m, :] for m in range(2)]
-            else:
-                accs = [psum.tile([P, P], F32, name="acc", tag="bank%d" % bank)[:] for bank in acc_banks[j]]
-            for m in range(N // P):
-                nc.tensor.matmul_mx(
-                    out=accs[m],
-                    lhsT=w_codes[:, m * P : (m + 1) * P].bitcast(FP8X4),
-                    lhsT_scale=w_scales[:, m * P : (m + 1) * P],
-                    rhs=x_codes[:, cols].bitcast(FP8X4),
-                    rhs_scale=x_scales[:, cols],
-                    start=True,
-                    stop=True,
-                )
-            nc.scalar.activation(out=result[:, j, 0, :], in_=accs[0], func=ACT.Relu, bias=bias[:, 0:1])
-            if j in (2, 0):
-                nc.scalar.activation(out=result[:, j, 1, :], in_=accs[1], func=ACT.Relu, bias=bias[:, 1:2])
-            else:
-                nc.vector.tensor_scalar(result[:, j, 1, :], accs[1], bias[:, 1:2], 0.0, ALU.add, ALU.max)
-            if j != 3:
-                nc.sync.dma_start(out=out_rows[:, :, cols], in_=result[:, j, :, :])
-            else:
-                nc.scalar.dma_start(out=out_rows[:, 0, cols], in_=result[:, j, 0, :])
-                nc.sync.dma_start(out=out_rows[:, 1, cols], in_=result[:, j, 1, :])
+        def product(acc, m, j):
+            nc.tensor.matmul_mx(
+                out=acc,
+                lhsT=w_codes[:, m * P : (m + 1) * P].bitcast(FP8X4),
+                lhsT_scale=w_scales[:, m * P : (m + 1) * P],
+                rhs=x_codes[:, j * P : (j + 1) * P].bitcast(FP8X4),
+                rhs_scale=x_scales[:, j * P : (j + 1) * P],
+                start=True,
+                stop=True,
+            )
+
+        def relu_scalar(acc, m, cols):
+            nc.scalar.activation(out=result[:, m, cols], in_=acc, func=ACT.Relu, bias=bias[:, m : m + 1])
+
+        def relu_vector(acc, m, cols):
+            nc.vector.tensor_scalar(result[:, m, cols], acc, bias[:, m : m + 1], 0.0, ALU.add, ALU.max)
+
+        for m, first, bank, relu in ((0, 2, 4, relu_scalar), (1, 2, 5, relu_vector), (0, 0, 2, relu_scalar)):
+            cols = slice(first * P, (first + 2) * P)
+            acc = psum.tile([P, 2 * P], F32, name="acc", tag="bank%d" % bank)
+            for i in range(2):
+                product(acc[:, i * P : (i + 1) * P], m, first + i)
+            relu(acc[:], m, cols)
+            nc.sync.dma_start(out=out[m * P : (m + 1) * P, cols], in_=result[:, m, cols])
+        for j, bank, relu in ((0, 0, relu_scalar), (1, 1, relu_vector)):
+            acc = psum.tile([P, P], F32, name="acc", tag="bank%d" % bank)
+            product(acc[:], 1, j)
+            relu(acc[:], 1, slice(j * P, (j + 1) * P))
+        nc.sync.dma_start(out=out[P : 2 * P, : 2 * P], in_=result[:, 1, : 2 * P])

@@ -36,12 +36,11 @@ def tile_picked_bag_lin_relu_sub_l_kernel(tc, xT, w, b, gate, offs, out):
         w_raw = keep.tile([P, PACK, N], F32, name="w_raw")
         bias = keep.tile([P, N // P], F32, name="bias")
         ident = keep.tile([P, P], F32, name="ident")
-        ident_bf = keep.tile([P, P], BF16, name="ident_bf")
         early = keep.tile([P, 2, D * V], F32, name="early")
         turned = keep.tile([P, V // P, P * 2], BF16, name="turned", tag="staging", align_bytes=64)
         turned_late = keep.tile([P, 2, P * 2], BF16, name="turned_late", tag="low_slot", align_bytes=64)
         x_bf0 = keep.tile([P, P * PACK], BF16, name="x_bf0", align_bytes=64)
-        last_pe = keep.tile([P, 2, D, P], F32, name="last_pe")
+        last_pe = keep.tile([P, D * 2 * P], F32, name="last_pe")
         late = keep.tile([P, LATE_WORDS], F32, name="late", align_bytes=64)
         x_bf1 = keep.tile([P, P * PACK], BF16, name="x_bf1", align_bytes=64)
         x_bf23 = keep.tile([P, 2 * P * PACK], BF16, name="x_bf23", align_bytes=64)
@@ -60,17 +59,17 @@ def tile_picked_bag_lin_relu_sub_l_kernel(tc, xT, w, b, gate, offs, out):
         with nc.allow_non_contiguous_dma(reason="one bias value to a partition"):
             nc.sync.dma_start(out=bias[:], in_=b.rearrange("(c p) o -> p (c o)", p=P))
 
-        make_identity(nc, ident_bf[:])
         make_identity(nc, ident[:])
         nc.vector.tensor_copy(out=gate_bf[:], in_=gate_cols[:, :, :PACK])
         for d in range(D):
-            spread = psum.tile([P, PACK, P], BF16, name="spread", tag="bank%d" % d)
-            for j in range(PACK):
-                nc.tensor.transpose(spread[:, j, :], gate_bf[:, d, j : j + 1].to_broadcast([P, P]), ident_bf[:])
+            spread = psum.tile([P, 2, P], F32, name="spread", tag="bank%d" % d)
+            for u in range(2):
+                word = gate_bf[:, d, :].bitcast(F32)[:, u : u + 1]
+                nc.tensor.transpose(spread[:, u, :], word.to_broadcast([P, P]), ident[:])
             copy_out = nc.vector.tensor_copy if d == 0 else nc.scalar.copy
             copy_out(
-                out=gates[:, d * V : (d + 1) * V].rearrange("m (p j) -> m p j", j=PACK),
-                in_=spread[:].rearrange("m j p -> m p j"),
+                out=gates[:, d * V : (d + 1) * V].rearrange("m (p u e) -> m p u e", u=2, e=2),
+                in_=spread[:].bitcast(BF16).rearrange("m u (p e) -> m p u e", e=2),
             )
 
         sums = [psum.tile([P, 4, P], F32, name="sums", tag="bank%d" % (2 + j)) for j in range(V // P)]
@@ -115,7 +114,7 @@ def tile_picked_bag_lin_relu_sub_l_kernel(tc, xT, w, b, gate, offs, out):
         w_bf = keep.tile([P, N * PACK], BF16, name="w_bf", tag="staging", align_bytes=64)
 
         def low_pairs(j):
-            sum_turned(sums[j][:, 3, :], [last_pe[:, j, d, :] for d in range(D)])
+            sum_turned(sums[j][:, 3, :], [last_pe[:, (2 * d + j) * P : (2 * d + j + 1) * P] for d in range(D)])
             round_pairs(turned_late[:, j, :], sums[j][:, 2:4, :])
             nc.tensor.transpose(words[j][:, 0, :], turned_late[:, j, :].bitcast(F32), ident[:])
 
@@ -143,9 +142,8 @@ def tile_picked_bag_lin_relu_sub_l_kernel(tc, xT, w, b, gate, offs, out):
                 out=x_codes[:, j * P : (j + 1) * P].bitcast(FP8X4), scales=x_scales[:, j * P : (j + 1) * P], in_=x_bf[j]
             )
 
-        for j in range(2):
-            for d in range(D):
-                gather(last_pe[:, j, d, :], 1, d * V + j * P, P)
+        for d in range(D):
+            gather(last_pe[:, d * 2 * P : (d + 1) * 2 * P], 1, d * V, 2 * P)
         low_pairs(0)
         nc.scalar.activation(
             out=w_bf[:].rearrange("p (c i t) -> p c t i", i=4, t=PACK),
@@ -155,10 +153,10 @@ def tile_picked_bag_lin_relu_sub_l_kernel(tc, xT, w, b, gate, offs, out):
         low_pairs(1)
         interleave(0)
         interleave(1)
-        gather(late[:, LAST_AT[2, 1] : LAST_AT[2, 1] + P], 1, V + 2 * P, P)
         gather(late[:, LAST_AT[2, 0] : LAST_AT[2, 0] + 2 * P], 1, 2 * P, 2 * P)
+        for j in (2, 3):
+            gather(late[:, LAST_AT[j, 1] : LAST_AT[j, 1] + P], 1, V + j * P, P)
         add(2)
-        gather(late[:, LAST_AT[3, 1] : LAST_AT[3, 1] + P], 1, V + 3 * P, P)
         quantize(2)
         add(3)
         w_codes = keep.tile([P, N], U32, name="w_codes", tag="low_slot", align_bytes=64)

@@ -19,7 +19,9 @@ P = 128
 PACK = 4
 HIGH_ORDER = (2, 3, 0, 1)
 LAST_AT = {(2, 0): D * V, (3, 0): D * V + P, (2, 1): D * V + 2 * P, (3, 1): D * V + 3 * P}
-LATE_WORDS = 2 * D * V - P
+W_AT = D * V + 4 * P
+LATE_WORDS = W_AT + PACK * N
+BAG = (2 * P, 3 * P, 0, P)
 
 
 def tile_picked_bag_lin_relu_sub_l_kernel(tc, xT, w, b, gate, offs, out):
@@ -33,18 +35,23 @@ def tile_picked_bag_lin_relu_sub_l_kernel(tc, xT, w, b, gate, offs, out):
         gate_cols = keep.tile([P, D, 2 * PACK], F32, name="gate_cols")
         gate_bf = keep.tile([P, D, PACK], BF16, name="gate_bf")
         gates = keep.tile([P, D * V], F32, name="gates")
-        w_raw = keep.tile([P, PACK, N], F32, name="w_raw")
         bias = keep.tile([P, N // P], F32, name="bias")
         ident = keep.tile([P, P], F32, name="ident")
         early = keep.tile([P, 2, D * V], F32, name="early")
-        turned = keep.tile([P, V // P, P * 2], BF16, name="turned", tag="staging", align_bytes=64)
-        turned_late = keep.tile([P, 2, P * 2], BF16, name="turned_late", tag="low_slot", align_bytes=64)
+        turned = [
+            keep.tile([P, 2, P * 2], BF16, name="turned01", tag="staging", align_bytes=64),
+            keep.tile([P, 2, P * 2], BF16, name="turned23", align_bytes=64),
+        ]
         x_bf0 = keep.tile([P, P * PACK], BF16, name="x_bf0", align_bytes=64)
         last_pe = keep.tile([P, D * 2 * P], F32, name="last_pe")
         late = keep.tile([P, LATE_WORDS], F32, name="late", align_bytes=64)
         x_bf1 = keep.tile([P, P * PACK], BF16, name="x_bf1", align_bytes=64)
         x_bf23 = keep.tile([P, 2 * P * PACK], BF16, name="x_bf23", align_bytes=64)
-        x_codes = keep.tile([P, V], U32, name="x_codes", align_bytes=64)
+        x_words = keep.tile([P, V], U32, name="x_words", align_bytes=64)
+        w_codes = keep.tile([P, N], U32, name="w_codes", align_bytes=64)
+        w_raw = late[:, W_AT:].rearrange("p (t c) -> p t c", t=PACK)
+        turned_late = [w_raw[:, 3, P:], w_raw[:, 2, P:]]
+        x_codes = [x_words[:, j * P : (j + 1) * P].bitcast(FP8X4) for j in range(V // P)]
         x_scales = keep.tile([P, V], U8, name="x_scales", align_bytes=64)
         w_scales = keep.tile([P, N], U8, name="w_scales", align_bytes=64)
         result = keep.tile([P, N // P, V], F32, name="result")
@@ -53,9 +60,12 @@ def tile_picked_bag_lin_relu_sub_l_kernel(tc, xT, w, b, gate, offs, out):
         nc.sync.dma_start(out=gate_cols[:, :, :PACK], in_=gate[:, 0, :].rearrange("d (p j) -> p d j", j=PACK))
         nc.sync.dma_start(out=planes[2][:], in_=x_rows[:, 2, :])
         nc.sync.dma_start(offsets[:], offs)
-        for t in (3, 0, 1):
+        w_rows = w.rearrange("(p t) c -> p (t c)", t=PACK)
+        for t in (3, 0):
             nc.sync.dma_start(out=planes[t][:], in_=x_rows[:, t, :])
-        nc.sync.dma_start(out=w_raw[:], in_=w.rearrange("(p t) c -> p t c", t=PACK))
+        nc.sync.dma_start(out=late[:, W_AT : W_AT + N], in_=w_rows[:, :N])
+        nc.sync.dma_start(out=planes[1][:], in_=x_rows[:, 1, :])
+        nc.sync.dma_start(out=late[:, W_AT + N :], in_=w_rows[:, N:])
         with nc.allow_non_contiguous_dma(reason="one bias value to a partition"):
             nc.sync.dma_start(out=bias[:], in_=b.rearrange("(c p) o -> p (c o)", p=P))
 
@@ -72,7 +82,7 @@ def tile_picked_bag_lin_relu_sub_l_kernel(tc, xT, w, b, gate, offs, out):
                 in_=spread[:].bitcast(BF16).rearrange("m u (p e) -> m p u e", e=2),
             )
 
-        sums = [psum.tile([P, 4, P], F32, name="sums", tag="bank%d" % (2 + j)) for j in range(V // P)]
+        high_sums = [psum.tile([P, 2, 2, P], F32, name="high_sums", tag="bank%d" % (4 + h)) for h in range(2)]
         words = [psum.tile([P, 2, P], F32, name="words", tag="bank%d" % bank) for bank in (6, 7, 0)]
 
         def gather(dst, t, e0, n):
@@ -93,30 +103,36 @@ def tile_picked_bag_lin_relu_sub_l_kernel(tc, xT, w, b, gate, offs, out):
             )
 
         for e in range(2):
-            gather(early[:, e, :], 2 + e, 0, D * V)
+            for e0, n in (((0, D * V),), ((0, V + 2 * P), (V + 2 * P, 2 * P)))[e]:
+                gather(early[:, e, e0 : e0 + n], 2 + e, e0, n)
             for j in HIGH_ORDER:
-                sum_turned(sums[j][:, e, :], [early[:, e, d * V + j * P : d * V + (j + 1) * P] for d in range(D)])
+                sum_turned(high_sums[j // 2][:, j % 2, e, :], [early[:, e, d * V + BAG[j] : d * V + BAG[j] + P] for d in range(D)])
         gather(late[:, : D * V], 0, 0, D * V)
 
-        for j in HIGH_ORDER:
-            round_pairs(turned[:, j, :], sums[j][:, 0:2, :])
-            high = words[j][:, 1, :] if j < 2 else words[2][:, j - 2, :]
-            nc.tensor.transpose(high, turned[:, j, :].bitcast(F32), ident[:])
+        for h in (1, 0):
+            nc.scalar.activation(
+                out=turned[h][:].rearrange("v j (p e) -> v j p e", e=2),
+                in_=high_sums[h][:].rearrange("v j e p -> v j p e"),
+                func=ACT.Copy,
+            )
+            for j in (2 * h, 2 * h + 1):
+                high = words[j][:, 1, :] if j < 2 else words[2][:, j - 2, :]
+                nc.tensor.transpose(high, turned[h][:, j % 2, :].bitcast(F32), ident[:])
         nc.scalar.copy(
             out=x_bf23[:].bitcast(F32).rearrange("p (v u) -> p v u", u=2),
             in_=words[2][:].rearrange("p j v -> p (j v)").unsqueeze(2).to_broadcast([P, 2 * P, 2]),
         )
 
+        low_sums = [psum.tile([P, 2, P], F32, name="low_sums", tag="bank%d" % bank) for bank in (4, 0)]
         for j in range(2):
-            sum_turned(sums[j][:, 2, :], [late[:, d * V + j * P : d * V + (j + 1) * P] for d in range(D)])
+            sum_turned(low_sums[j][:, 0, :], [late[:, d * V + BAG[j] : d * V + BAG[j] + P] for d in range(D)])
 
         x_bf = [x_bf0[:], x_bf1[:], x_bf23[:, : P * PACK], x_bf23[:, P * PACK :]]
         w_bf = keep.tile([P, N * PACK], BF16, name="w_bf", tag="staging", align_bytes=64)
 
         def low_pairs(j):
-            sum_turned(sums[j][:, 3, :], [last_pe[:, (2 * d + j) * P : (2 * d + j + 1) * P] for d in range(D)])
-            round_pairs(turned_late[:, j, :], sums[j][:, 2:4, :])
-            nc.tensor.transpose(words[j][:, 0, :], turned_late[:, j, :].bitcast(F32), ident[:])
+            round_pairs(turned_late[j].bitcast(BF16), low_sums[j][:])
+            nc.tensor.transpose(words[j][:, 0, :], turned_late[j], ident[:])
 
         def interleave(j):
             nc.scalar.copy(
@@ -125,7 +141,7 @@ def tile_picked_bag_lin_relu_sub_l_kernel(tc, xT, w, b, gate, offs, out):
 
         def add(j):
             def planes_0_1(d):
-                first = d * V + j * P
+                first = d * V + BAG[j]
                 apart = LAST_AT[j, d] - first
                 both = late[:, first : first + 2 * apart].rearrange("p (e s) -> p e s", e=2)[:, :, :P]
                 return both.rearrange("p e (c i) -> p c e i", i=2)
@@ -139,34 +155,50 @@ def tile_picked_bag_lin_relu_sub_l_kernel(tc, xT, w, b, gate, offs, out):
 
         def quantize(j):
             nc.vector.quantize_mx(
-                out=x_codes[:, j * P : (j + 1) * P].bitcast(FP8X4), scales=x_scales[:, j * P : (j + 1) * P], in_=x_bf[j]
+                out=x_codes[j], scales=x_scales[:, j * P : (j + 1) * P], in_=x_bf[j]
             )
 
-        for d in range(D):
-            gather(last_pe[:, d * 2 * P : (d + 1) * 2 * P], 1, d * V, 2 * P)
-        low_pairs(0)
-        nc.scalar.activation(
-            out=w_bf[:].rearrange("p (c i t) -> p c t i", i=4, t=PACK),
-            in_=w_raw[:].rearrange("p t (c i) -> p c t i", i=4),
-            func=ACT.Copy,
-        )
-        low_pairs(1)
-        interleave(0)
-        interleave(1)
-        gather(late[:, LAST_AT[2, 0] : LAST_AT[2, 0] + 2 * P], 1, 2 * P, 2 * P)
-        for j in (2, 3):
-            gather(late[:, LAST_AT[j, 1] : LAST_AT[j, 1] + P], 1, V + j * P, P)
-        add(2)
-        quantize(2)
-        add(3)
-        w_codes = keep.tile([P, N], U32, name="w_codes", tag="low_slot", align_bytes=64)
-        for m, j in ((0, 3), (1, 0)):
+        def cast_w(m):
+            nc.scalar.activation(
+                out=w_bf[:, m * P * PACK : (m + 1) * P * PACK].rearrange("p (c i t) -> p c t i", i=4, t=PACK),
+                in_=w_raw[:, :, m * P : (m + 1) * P].rearrange("p t (c i) -> p c t i", i=4),
+                func=ACT.Copy,
+            )
+
+        def quantize_w(m):
             nc.vector.quantize_mx(
                 out=w_codes[:, m * P : (m + 1) * P].bitcast(FP8X4),
                 scales=w_scales[:, m * P : (m + 1) * P],
                 in_=w_bf[:, m * P * PACK : (m + 1) * P * PACK],
             )
-            quantize(j)
+
+        for d in range(D):
+            gather(last_pe[:, d * 2 * P : (d + 1) * 2 * P], 1, d * V + BAG[0], 2 * P)
+            for j in range(2):
+                piece = last_pe[:, (2 * d + j) * P : (2 * d + j + 1) * P]
+                nc.tensor.matmul(
+                    low_sums[j][:, 1, :], piece, ident[:], start=(d == 0), stop=(d == D - 1), is_transpose=True
+                )
+        cast_w(0)
+        cast_w(1)
+        low_pairs(0)
+        low_pairs(1)
+        interleave(0)
+        interleave(1)
+
+        def gather_last(j, d):
+            gather(late[:, LAST_AT[j, d] : LAST_AT[j, d] + P], 1, d * V + BAG[j], P)
+
+        gather(late[:, LAST_AT[2, 0] : LAST_AT[2, 0] + 2 * P], 1, BAG[2], 2 * P)
+        gather_last(2, 1)
+        gather_last(3, 1)
+        add(2)
+        add(3)
+        quantize_w(0)
+        quantize(2)
+        quantize_w(1)
+        quantize(3)
+        quantize(0)
         quantize(1)
 
         def product(acc, m, j):
@@ -174,7 +206,7 @@ def tile_picked_bag_lin_relu_sub_l_kernel(tc, xT, w, b, gate, offs, out):
                 out=acc,
                 lhsT=w_codes[:, m * P : (m + 1) * P].bitcast(FP8X4),
                 lhsT_scale=w_scales[:, m * P : (m + 1) * P],
-                rhs=x_codes[:, j * P : (j + 1) * P].bitcast(FP8X4),
+                rhs=x_codes[j],
                 rhs_scale=x_scales[:, j * P : (j + 1) * P],
                 start=True,
                 stop=True,
@@ -186,15 +218,17 @@ def tile_picked_bag_lin_relu_sub_l_kernel(tc, xT, w, b, gate, offs, out):
         def relu_vector(acc, m, cols):
             nc.vector.tensor_scalar(result[:, m, cols], acc, bias[:, m : m + 1], 0.0, ALU.add, ALU.max)
 
-        for m, first, bank, relu in ((0, 2, 4, relu_scalar), (1, 2, 5, relu_vector), (0, 0, 2, relu_scalar)):
-            cols = slice(first * P, (first + 2) * P)
-            acc = psum.tile([P, 2 * P], F32, name="acc", tag="bank%d" % bank)
-            for i in range(2):
-                product(acc[:, i * P : (i + 1) * P], m, first + i)
-            relu(acc[:], m, cols)
-            nc.sync.dma_start(out=out[m * P : (m + 1) * P, cols], in_=result[:, m, cols])
-        for j, bank, relu in ((0, 0, relu_scalar), (1, 1, relu_vector)):
-            acc = psum.tile([P, P], F32, name="acc", tag="bank%d" % bank)
-            product(acc[:], 1, j)
-            relu(acc[:], 1, slice(j * P, (j + 1) * P))
-        nc.sync.dma_start(out=out[P : 2 * P, : 2 * P], in_=result[:, 1, : 2 * P])
+        relus = (relu_scalar, relu_vector)
+        accs = [psum.tile([P, 2 * P], F32, name="acc", tag="bank%d" % bank) for bank in (0, 6)]
+        for m, i in ((0, 0), (1, 0), (1, 1), (0, 1)):
+            product(accs[m][:, i * P : (i + 1) * P], m, 2 + i)
+        for m in range(2):
+            relus[m](accs[m][:], m, slice(0, 2 * P))
+            nc.sync.dma_start(out=out[m * P : (m + 1) * P, : 2 * P], in_=result[:, m, : 2 * P])
+        for j, banks in ((0, (2, 3)), (1, (1, 5))):
+            for m in (j, 1 - j):
+                acc = psum.tile([P, P], F32, name="acc", tag="bank%d" % banks[m])
+                product(acc[:], m, j)
+                relus[m](acc[:], m, slice(BAG[j], BAG[j] + P))
+        for m in range(2):
+            nc.sync.dma_start(out=out[m * P : (m + 1) * P, 2 * P :], in_=result[:, m, 2 * P :])

@@ -17,7 +17,8 @@ ACT = mybir.ActivationFunctionType
 
 P = 128
 PACK = 4
-HIGH_ORDER = (2, 3, 0, 1)
+HIGH_ORDER = (2, 3, 0)
+VV = 3 * P
 LAST_AT = {(2, 0): D * V, (3, 0): D * V + P, (2, 1): D * V + 2 * P, (3, 1): D * V + 3 * P}
 W_AT = D * V + 4 * P
 LATE_WORDS = W_AT + PACK * N
@@ -35,13 +36,18 @@ def tile_picked_bag_lin_relu_sub_l_kernel(tc, xT, w, b, gate, offs, out):
         gate_cols = keep.tile([P, D, 2 * PACK], F32, name="gate_cols")
         gate_bf = keep.tile([P, D, PACK], BF16, name="gate_bf")
         gates = keep.tile([P, D * V], F32, name="gates")
+        gate_of_bag = keep.tile([P, D], F32, name="gate_of_bag")
+        ident_bf = keep.tile([P, P], BF16, name="ident_bf")
         bias = keep.tile([P, N // P], F32, name="bias")
         ident = keep.tile([P, P], F32, name="ident")
-        early = keep.tile([P, 2, D * V], F32, name="early")
-        turned = [
-            keep.tile([P, 2, P * 2], BF16, name="turned01", tag="staging", align_bytes=64),
-            keep.tile([P, 2, P * 2], BF16, name="turned23", align_bytes=64),
+        early_all = keep.tile([P, 4 * VV + P // 2 + P], F32, name="early_all")
+        early = [
+            [early_all[:, 2 * VV + P // 2 : 3 * VV + P // 2], early_all[:, 3 * VV + P // 2 : 4 * VV + P // 2]],
+            [early_all[:, VV : 2 * VV], early_all[:, :VV]],
         ]
+        picks_at = (2 * VV - P // 2, 4 * VV + P // 2)
+        turned0 = keep.tile([P, P * 2], BF16, name="turned0", tag="staging", align_bytes=64)
+        turned23 = keep.tile([P, 2, P * 2], BF16, name="turned23", align_bytes=64)
         x_bf0 = keep.tile([P, P * PACK], BF16, name="x_bf0", align_bytes=64)
         last_pe = keep.tile([P, D * 2 * P], F32, name="last_pe")
         late = keep.tile([P, LATE_WORDS], F32, name="late", align_bytes=64)
@@ -49,6 +55,7 @@ def tile_picked_bag_lin_relu_sub_l_kernel(tc, xT, w, b, gate, offs, out):
         x_bf23 = keep.tile([P, 2 * P * PACK], BF16, name="x_bf23", align_bytes=64)
         x_words = keep.tile([P, V], U32, name="x_words", align_bytes=64)
         w_codes = keep.tile([P, N], U32, name="w_codes", align_bytes=64)
+        turned = [turned0[:], last_pe[:, 3 * P // 2 : 5 * P // 2].bitcast(BF16), turned23[:, 0, :], turned23[:, 1, :]]
         w_raw = late[:, W_AT:].rearrange("p (t c) -> p t c", t=PACK)
         turned_late = [w_raw[:, 3, P:], w_raw[:, 2, P:]]
         x_codes = [x_words[:, j * P : (j + 1) * P].bitcast(FP8X4) for j in range(V // P)]
@@ -70,9 +77,12 @@ def tile_picked_bag_lin_relu_sub_l_kernel(tc, xT, w, b, gate, offs, out):
             nc.sync.dma_start(out=bias[:], in_=b.rearrange("(c p) o -> p (c o)", p=P))
 
         make_identity(nc, ident[:])
+        make_identity(nc, ident_bf[:])
         nc.vector.tensor_copy(out=gate_bf[:], in_=gate_cols[:, :, :PACK])
+        spreads = []
         for d in range(D):
-            spread = psum.tile([P, 2, P], F32, name="spread", tag="bank%d" % d)
+            spread = psum.tile([P, 2, P], F32, name="spread", tag="bank%d" % (4 + d))
+            spreads.append(spread)
             for u in range(2):
                 word = gate_bf[:, d, :].bitcast(F32)[:, u : u + 1]
                 nc.tensor.transpose(spread[:, u, :], word.to_broadcast([P, P]), ident[:])
@@ -82,7 +92,19 @@ def tile_picked_bag_lin_relu_sub_l_kernel(tc, xT, w, b, gate, offs, out):
                 in_=spread[:].bitcast(BF16).rearrange("m u (p e) -> m p u e", e=2),
             )
 
+        gate_turned = psum.tile([P, D, P], BF16, name="gate_turned", tag="bank2")
+        for d in (1, 0):
+            at = picks_at[1 - d] + P // 4
+            columns = early_all[:, at : at + P // 2].bitcast(BF16)
+            nc.scalar.copy(
+                out=columns.rearrange("m (p u e) -> m p u e", u=2, e=2),
+                in_=spreads[d][:].bitcast(BF16).rearrange("m u (p e) -> m p u e", e=2)[:, BAG[1] // PACK :],
+            )
+            nc.tensor.transpose(gate_turned[:, d, :], columns, ident_bf[:])
+        nc.scalar.copy(out=gate_of_bag[:], in_=gate_turned[:, :, 0])
+
         high_sums = [psum.tile([P, 2, 2, P], F32, name="high_sums", tag="bank%d" % (4 + h)) for h in range(2)]
+        high_picked = [psum.tile([P, 2, P], BF16, name="high_picked", tag="bank%d" % bank) for bank in (3, 1)]
         words = [psum.tile([P, 2, P], F32, name="words", tag="bank%d" % bank) for bank in (6, 7, 0)]
 
         def gather(dst, t, e0, n):
@@ -102,22 +124,45 @@ def tile_picked_bag_lin_relu_sub_l_kernel(tc, xT, w, b, gate, offs, out):
                 out=dst.rearrange("v (p e) -> v p e", e=2), in_=src.rearrange("v e p -> v p e"), func=ACT.Copy
             )
 
+        scaled = late[:, D * V - P // 2 : D * V - P // 2 + 6 * P].rearrange("v (e s) -> v e s", e=2)[:, :, :P]
+
+        def pick(t, e):
+            for d in (1, 0):
+                e0 = d * V + BAG[1]
+                at = picks_at[e] + d * P // 2
+                picked = early_all[:, at : at + P // 2].bitcast(BF16)
+                nc.scalar.activation(
+                    out=picked, in_=planes[t][:].indirect(offsets[:, e0 // 16 : (e0 + P) // 16]), func=ACT.Copy
+                )
+                nc.tensor.transpose(high_picked[d][:, e, :], picked, ident_bf[:])
+            nc.scalar.activation(out=scaled[:, e, :], in_=high_picked[1][:, e, :], func=ACT.Copy, scale=gate_of_bag[:, 1:2])
+
         for e in range(2):
-            for e0, n in (((0, D * V),), ((0, V + 2 * P), (V + 2 * P, 2 * P)))[e]:
-                gather(early[:, e, e0 : e0 + n], 2 + e, e0, n)
+            pick(2 + e, e)
+            for d in ((0, 1), (1, 0))[e]:
+                gather(early[e][d], 2 + e, d * V, VV)
             for j in HIGH_ORDER:
-                sum_turned(high_sums[j // 2][:, j % 2, e, :], [early[:, e, d * V + BAG[j] : d * V + BAG[j] + P] for d in range(D)])
+                sum_turned(high_sums[j // 2][:, j % 2, e, :], [early[e][d][:, BAG[j] : BAG[j] + P] for d in range(D)])
+        nc.vector.scalar_tensor_tensor(
+            turned[1].rearrange("v (p e) -> v p e", e=2),
+            high_picked[0][:].rearrange("v e p -> v p e"),
+            gate_of_bag[:, 0:1],
+            scaled.rearrange("v e p -> v p e"),
+            ALU.mult,
+            ALU.add,
+        )
         gather(late[:, : D * V], 0, 0, D * V)
 
-        for h in (1, 0):
-            nc.scalar.activation(
-                out=turned[h][:].rearrange("v j (p e) -> v j p e", e=2),
-                in_=high_sums[h][:].rearrange("v j e p -> v j p e"),
-                func=ACT.Copy,
-            )
-            for j in (2 * h, 2 * h + 1):
-                high = words[j][:, 1, :] if j < 2 else words[2][:, j - 2, :]
-                nc.tensor.transpose(high, turned[h][:, j % 2, :].bitcast(F32), ident[:])
+        nc.scalar.activation(
+            out=turned23[:].rearrange("v j (p e) -> v j p e", e=2),
+            in_=high_sums[1][:].rearrange("v j e p -> v j p e"),
+            func=ACT.Copy,
+        )
+        for j in (2, 3):
+            nc.tensor.transpose(words[2][:, j - 2, :], turned[j].bitcast(F32), ident[:])
+        round_pairs(turned[0], high_sums[0][:, 0, :, :])
+        for j in (0, 1):
+            nc.tensor.transpose(words[j][:, 1, :], turned[j].bitcast(F32), ident[:])
         nc.scalar.copy(
             out=x_bf23[:].bitcast(F32).rearrange("p (v u) -> p v u", u=2),
             in_=words[2][:].rearrange("p j v -> p (j v)").unsqueeze(2).to_broadcast([P, 2 * P, 2]),

@@ -70,9 +70,8 @@ def tile_picked_bag_lin_relu_sub_l_kernel(tc, xT, w, b, gate, offs, out):
         w_rows = w.rearrange("(p t) c -> p (t c)", t=PACK)
         for t in (3, 0):
             nc.sync.dma_start(out=planes[t][:], in_=x_rows[:, t, :])
-        nc.sync.dma_start(out=late[:, W_AT : W_AT + N], in_=w_rows[:, :N])
         nc.sync.dma_start(out=planes[1][:], in_=x_rows[:, 1, :])
-        nc.sync.dma_start(out=late[:, W_AT + N :], in_=w_rows[:, N:])
+        nc.sync.dma_start(out=late[:, W_AT:], in_=w_rows)
         with nc.allow_non_contiguous_dma(reason="one bias value to a partition"):
             nc.sync.dma_start(out=bias[:], in_=b.rearrange("(c p) o -> p (c o)", p=P))
 

@@ -17,12 +17,10 @@ ACT = mybir.ActivationFunctionType
 
 P = 128
 PACK = 4
-HIGH_ORDER = (2, 3, 0)
-VV = 3 * P
-LAST_AT = {(2, 0): D * V, (3, 0): D * V + P, (2, 1): D * V + 2 * P, (3, 1): D * V + 3 * P}
-W_AT = D * V + 4 * P
-LATE_WORDS = W_AT + PACK * N
-BAG = (2 * P, 3 * P, 0, P)
+H = V // 2
+PLANES = (2, 3, 0, 1)
+STEP = D * H
+PICKS = PACK * STEP
 
 
 def tile_picked_bag_lin_relu_sub_l_kernel(tc, xT, w, b, gate, offs, out):
@@ -35,211 +33,174 @@ def tile_picked_bag_lin_relu_sub_l_kernel(tc, xT, w, b, gate, offs, out):
         planes = [keep.tile([P, T], F32, name="plane%d" % t) for t in range(PACK)]
         gate_cols = keep.tile([P, D, 2 * PACK], F32, name="gate_cols")
         gate_bf = keep.tile([P, D, PACK], BF16, name="gate_bf")
-        gates = keep.tile([P, D * V], F32, name="gates")
-        gate_of_bag = keep.tile([P, D], F32, name="gate_of_bag")
+        gates = keep.tile([P, D * H], F32, name="gates")
         ident_bf = keep.tile([P, P], BF16, name="ident_bf")
-        bias = keep.tile([P, N // P], F32, name="bias")
         ident = keep.tile([P, P], F32, name="ident")
-        early_all = keep.tile([P, 4 * VV + P // 2 + P], F32, name="early_all")
-        early = [
-            [early_all[:, 2 * VV + P // 2 : 3 * VV + P // 2], early_all[:, 3 * VV + P // 2 : 4 * VV + P // 2]],
-            [early_all[:, VV : 2 * VV], early_all[:, :VV]],
-        ]
-        picks_at = (2 * VV - P // 2, 4 * VV + P // 2)
-        turned0 = keep.tile([P, P * 2], BF16, name="turned0", tag="staging", align_bytes=64)
-        turned23 = keep.tile([P, 2, P * 2], BF16, name="turned23", align_bytes=64)
-        x_bf0 = keep.tile([P, P * PACK], BF16, name="x_bf0", align_bytes=64)
-        last_pe = keep.tile([P, D * 2 * P], F32, name="last_pe")
-        late = keep.tile([P, LATE_WORDS], F32, name="late", align_bytes=64)
-        x_bf1 = keep.tile([P, P * PACK], BF16, name="x_bf1", align_bytes=64)
-        x_bf23 = keep.tile([P, 2 * P * PACK], BF16, name="x_bf23", align_bytes=64)
-        x_words = keep.tile([P, V], U32, name="x_words", align_bytes=64)
+        bias = keep.tile([P, N // P], F32, name="bias")
+        work = keep.tile([P, PICKS + 6 * H], F32, name="work", align_bytes=64)
+        turned_b = keep.tile([P, 2, 2 * P], BF16, name="turned_b")
+        x_picked = [keep.tile([P, P * PACK], BF16, name="x_picked%d" % j, align_bytes=64) for j in range(2)]
+        x_added = keep.tile([P, 2 * P * PACK + 16], BF16, name="x_added", align_bytes=64)
+        w_raw = keep.tile([P, PACK, N], F32, name="w_raw")
+        w_bf = [work[:, at : at + H].bitcast(BF16) for at in (PICKS + PACK * H + P, PICKS + PACK * H - P)]
+        low_scaled = keep.tile([P, D * H], F32, name="low_scaled", tag="late", align_bytes=64)
         w_codes = keep.tile([P, N], U32, name="w_codes", align_bytes=64)
-        turned = [turned0[:], last_pe[:, 3 * P // 2 : 5 * P // 2].bitcast(BF16), turned23[:, 0, :], turned23[:, 1, :]]
-        w_raw = late[:, W_AT:].rearrange("p (t c) -> p t c", t=PACK)
-        turned_late = [w_raw[:, 3, P:], w_raw[:, 2, P:]]
-        x_codes = [x_words[:, j * P : (j + 1) * P].bitcast(FP8X4) for j in range(V // P)]
         x_scales = keep.tile([P, V], U8, name="x_scales", align_bytes=64)
         w_scales = keep.tile([P, N], U8, name="w_scales", align_bytes=64)
         result = keep.tile([P, N // P, V], F32, name="result")
 
         x_rows = xT.rearrange("(p t) c -> p t c", t=PACK)
         nc.sync.dma_start(out=gate_cols[:, :, :PACK], in_=gate[:, 0, :].rearrange("d (p j) -> p d j", j=PACK))
-        nc.sync.dma_start(out=planes[2][:], in_=x_rows[:, 2, :])
+        nc.sync.dma_start(out=planes[PLANES[0]][:], in_=x_rows[:, PLANES[0], :])
         nc.sync.dma_start(offsets[:], offs)
-        w_rows = w.rearrange("(p t) c -> p (t c)", t=PACK)
-        for t in (3, 0):
+        for t in PLANES[1:]:
             nc.sync.dma_start(out=planes[t][:], in_=x_rows[:, t, :])
-        nc.sync.dma_start(out=planes[1][:], in_=x_rows[:, 1, :])
-        nc.sync.dma_start(out=late[:, W_AT:], in_=w_rows)
+        nc.sync.dma_start(out=w_raw[:], in_=w.rearrange("(p t) c -> p t c", t=PACK))
         with nc.allow_non_contiguous_dma(reason="one bias value to a partition"):
             nc.sync.dma_start(out=bias[:], in_=b.rearrange("(c p) o -> p (c o)", p=P))
 
+        def products(n, d):
+            return work[:, n * STEP + d * H : n * STEP + (d + 1) * H]
+
+        def picks_at(n):
+            return STEP + P if n == 0 else PICKS + n * H
+
+        def picks(n, d, j):
+            at = picks_at(n) + (2 * d + j) * P // 2
+            return work[:, at : at + P // 2].bitcast(BF16)
+
+        def scaled(u, j):
+            if u == 0:
+                return low_scaled[:, j * H : (j + 1) * H].rearrange("v (e s) -> v e s", e=2)
+            at = (2 + j) * STEP + H - P // 2
+            return work[:, at : at + H].rearrange("v (e s) -> v e s", e=2)
+
+        gate_rows = work[:, PICKS : PICKS + H].bitcast(BF16)
+        turned = [
+            [gates[:, 3 * P :].bitcast(BF16), work[:, :P].bitcast(BF16)],
+            [turned_b[:, 0, :], turned_b[:, 1, :]],
+        ]
         make_identity(nc, ident[:])
         make_identity(nc, ident_bf[:])
-        nc.vector.tensor_copy(out=gate_bf[:], in_=gate_cols[:, :, :PACK])
-        spreads = []
+        nc.scalar.activation(out=gate_bf[:], in_=gate_cols[:, :, :PACK], func=ACT.Copy)
+        spread = psum.tile([P, D, 2, P], F32, name="spread", tag="bank0")
         for d in range(D):
-            spread = psum.tile([P, 2, P], F32, name="spread", tag="bank%d" % (4 + d))
-            spreads.append(spread)
             for u in range(2):
                 word = gate_bf[:, d, :].bitcast(F32)[:, u : u + 1]
-                nc.tensor.transpose(spread[:, u, :], word.to_broadcast([P, P]), ident[:])
-            copy_out = nc.vector.tensor_copy if d == 0 else nc.scalar.copy
-            copy_out(
-                out=gates[:, d * V : (d + 1) * V].rearrange("m (p u e) -> m p u e", u=2, e=2),
-                in_=spread[:].bitcast(BF16).rearrange("m u (p e) -> m p u e", e=2),
-            )
-
-        gate_turned = psum.tile([P, D, P], BF16, name="gate_turned", tag="bank2")
+                nc.tensor.transpose(spread[:, d, u, :], word.to_broadcast([P, P]), ident[:])
+        by_bag = spread[:].bitcast(BF16).rearrange("m d u (p e) -> m d p u e", e=2)
+        for dst, half in ((gate_rows, by_bag[:, :, : P // 2]), (gates[:], by_bag[:, :, P // 2 :])):
+            nc.vector.tensor_copy(out=dst.rearrange("m (d p u e) -> m d p u e", d=D, u=2, e=2), in_=half)
+        gate_turned = [psum.tile([P, 2, P], BF16, name="gate_turned", tag="bank%d" % (2 + d)) for d in range(D)]
         for d in (1, 0):
-            at = picks_at[1 - d] + P // 4
-            columns = early_all[:, at : at + P // 2].bitcast(BF16)
-            nc.scalar.copy(
-                out=columns.rearrange("m (p u e) -> m p u e", u=2, e=2),
-                in_=spreads[d][:].bitcast(BF16).rearrange("m u (p e) -> m p u e", e=2)[:, BAG[1] // PACK :],
-            )
-            nc.tensor.transpose(gate_turned[:, d, :], columns, ident_bf[:])
-        nc.scalar.copy(out=gate_of_bag[:], in_=gate_turned[:, :, 0])
+            for j in range(2):
+                at = d * H + j * P
+                nc.tensor.transpose(gate_turned[d][:, j if d == 0 else 1 - j, :], gate_rows[:, at : at + P], ident_bf[:])
+        gate0 = x_added[:].bitcast(F32)[:, 2 * P : 4 * P + 1 : 2 * P]
+        at = PICKS + 2 * H
+        gate1 = work[:, at : at + 3 * H : P].rearrange("p (n j) -> p n j", n=3)
+        nc.vector.tensor_copy(out=gate1, in_=gate_turned[1][:, :, 0].unsqueeze(1).to_broadcast([P, 3, 2]))
+        nc.vector.tensor_copy(out=gate0, in_=gate_turned[0][:, :, 0])
 
-        high_sums = [psum.tile([P, 2, 2, P], F32, name="high_sums", tag="bank%d" % (4 + h)) for h in range(2)]
-        high_picked = [psum.tile([P, 2, P], BF16, name="high_picked", tag="bank%d" % bank) for bank in (3, 1)]
-        words = [psum.tile([P, 2, P], F32, name="words", tag="bank%d" % bank) for bank in (6, 7, 0)]
+        words = [psum.tile([P, 2, P], F32, name="words", tag="bank%d" % (6 + j)) for j in range(2)]
 
-        def gather(dst, t, e0, n):
-            nc.vector.tensor_tensor(
-                dst,
-                planes[t][:].indirect(offsets[:, e0 // 16 : (e0 + n) // 16]),
-                gates[:, e0 : e0 + n],
-                ALU.mult,
-            )
+        def window(t, e0, count):
+            return planes[t][:].indirect(offsets[:, e0 // 16 : (e0 + count) // 16])
 
-        def sum_turned(dst, pieces):
-            for d in range(D):
-                nc.tensor.matmul(dst, pieces[d], ident[:], start=(d == 0), stop=(d == D - 1), is_transpose=True)
+        def add(n, j, count=1):
+            def both(d):
+                at = (n - 1) * STEP + d * H + j * P
+                pair = work[:, at : at + 2 * STEP].rearrange("p (e s) -> p e s", e=2)[:, :, : count * P]
+                return pair.rearrange("p e (c i) -> p c e i", i=2)
 
-        def round_pairs(dst, src):
-            nc.scalar.activation(
-                out=dst.rearrange("v (p e) -> v p e", e=2), in_=src.rearrange("v e p -> v p e"), func=ACT.Copy
-            )
+            t = PLANES[n - 1]
+            dst = x_added[:, j * P * PACK : (j + count) * P * PACK].rearrange("p (c i t) -> p c t i", i=2, t=PACK)
+            nc.vector.tensor_tensor(dst[:, :, t : t + 2, :], both(0), both(1), ALU.add)
 
-        scaled = late[:, D * V - P // 2 : D * V - P // 2 + 6 * P].rearrange("v (e s) -> v e s", e=2)[:, :, :P]
-
-        def pick(t, e):
+        for n, t in enumerate(PLANES):
+            u, e = t // 2, t % 2
+            if e == 0:
+                flipped = {}
+                for d in range(D):
+                    if u == 1 or d == 1:
+                        both_tiles = psum.tile([P, 2, 2, P], BF16, name="flipped", tag="bank%d" % (2 + d))
+                    for j in range(2):
+                        if u == 1 or d == 1:
+                            flipped[j, d] = both_tiles[:, j]
+                        else:
+                            one = psum.tile([P, 2, P], BF16, name="flipped", tag="bank%d" % (2 + 2 * j + d))
+                            flipped[j, d] = one[:]
             for d in (1, 0):
-                e0 = d * V + BAG[1]
-                at = picks_at[e] + d * P // 2
-                picked = early_all[:, at : at + P // 2].bitcast(BF16)
-                nc.scalar.activation(
-                    out=picked, in_=planes[t][:].indirect(offsets[:, e0 // 16 : (e0 + P) // 16]), func=ACT.Copy
+                at = picks_at(n) + d * P
+                nc.scalar.activation(out=work[:, at : at + P].bitcast(BF16), in_=window(t, d * V, H), func=ACT.Copy)
+                for j in range(2):
+                    nc.tensor.transpose(flipped[j, d][:, e, :], picks(n, d, j), ident_bf[:])
+            for d, first, count in ((0, 0, H), (1, 0, P), (1, P, P)) if n == PACK - 1 else ((0, 0, H), (1, 0, H)):
+                nc.vector.tensor_tensor(
+                    products(n, d)[:, first : first + count],
+                    window(t, d * V + H + first, count),
+                    gates[:, d * H + first : d * H + first + count],
+                    ALU.mult,
                 )
-                nc.tensor.transpose(high_picked[d][:, e, :], picked, ident_bf[:])
-            nc.scalar.activation(out=scaled[:, e, :], in_=high_picked[1][:, e, :], func=ACT.Copy, scale=gate_of_bag[:, 1:2])
+            if n == 1:
+                add(n, 0)
+                add(n, 1)
+            if n == PACK - 1:
+                add(n, 0)
+            for j in range(2):
+                if n > 0:
+                    part = slice(0, 2) if u == 1 else slice(e, e + 1)
+                    nc.scalar.activation(
+                        out=scaled(u, j)[:, part],
+                        in_=flipped[j, 1][:, part],
+                        func=ACT.Copy,
+                        scale=gate1[:, n - 1, 1 - j : 2 - j],
+                    )
+                if e == 1:
+                    nc.vector.scalar_tensor_tensor(
+                        turned[j][u].rearrange("v (p e) -> v p e", e=2),
+                        flipped[j, 0].rearrange("v e p -> v p e"),
+                        gate0[:, j : j + 1],
+                        scaled(u, j).rearrange("v e p -> v p e"),
+                        ALU.mult,
+                        ALU.add,
+                    )
+                    nc.tensor.transpose(words[j][:, u, :], turned[j][u].bitcast(F32), ident[:])
 
-        for e in range(2):
-            pick(2 + e, e)
-            for d in ((0, 1), (1, 0))[e]:
-                gather(early[e][d], 2 + e, d * V, VV)
-            for j in HIGH_ORDER:
-                sum_turned(high_sums[j // 2][:, j % 2, e, :], [early[e][d][:, BAG[j] : BAG[j] + P] for d in range(D)])
-        nc.vector.scalar_tensor_tensor(
-            turned[1].rearrange("v (p e) -> v p e", e=2),
-            high_picked[0][:].rearrange("v e p -> v p e"),
-            gate_of_bag[:, 0:1],
-            scaled.rearrange("v e p -> v p e"),
-            ALU.mult,
-            ALU.add,
-        )
-        gather(late[:, : D * V], 0, 0, D * V)
+        x_words = keep.tile([P, V], U32, name="x_words", tag="late", align_bytes=64)
+        x_bf = [x_picked[0][:], x_picked[1][:], x_added[:, : P * PACK], x_added[:, P * PACK : 2 * P * PACK]]
 
-        nc.scalar.activation(
-            out=turned23[:].rearrange("v j (p e) -> v j p e", e=2),
-            in_=high_sums[1][:].rearrange("v j e p -> v j p e"),
-            func=ACT.Copy,
-        )
-        for j in (2, 3):
-            nc.tensor.transpose(words[2][:, j - 2, :], turned[j].bitcast(F32), ident[:])
-        round_pairs(turned[0], high_sums[0][:, 0, :, :])
-        for j in (0, 1):
-            nc.tensor.transpose(words[j][:, 1, :], turned[j].bitcast(F32), ident[:])
-        nc.scalar.copy(
-            out=x_bf23[:].bitcast(F32).rearrange("p (v u) -> p v u", u=2),
-            in_=words[2][:].rearrange("p j v -> p (j v)").unsqueeze(2).to_broadcast([P, 2 * P, 2]),
-        )
-
-        low_sums = [psum.tile([P, 2, P], F32, name="low_sums", tag="bank%d" % bank) for bank in (4, 0)]
-        for j in range(2):
-            sum_turned(low_sums[j][:, 0, :], [late[:, d * V + BAG[j] : d * V + BAG[j] + P] for d in range(D)])
-
-        x_bf = [x_bf0[:], x_bf1[:], x_bf23[:, : P * PACK], x_bf23[:, P * PACK :]]
-        w_bf = keep.tile([P, N * PACK], BF16, name="w_bf", tag="staging", align_bytes=64)
-
-        def low_pairs(j):
-            round_pairs(turned_late[j].bitcast(BF16), low_sums[j][:])
-            nc.tensor.transpose(words[j][:, 0, :], turned_late[j], ident[:])
+        def cast_w(m):
+            nc.scalar.activation(
+                out=w_bf[m].rearrange("p (c i t) -> p c t i", i=4, t=PACK),
+                in_=w_raw[:, :, m * P : (m + 1) * P].rearrange("p t (c i) -> p c t i", i=4),
+                func=ACT.Copy,
+            )
 
         def interleave(j):
             nc.scalar.copy(
                 out=x_bf[j].bitcast(F32).rearrange("p (v u) -> p v u", u=2), in_=words[j][:].rearrange("p u v -> p v u")
             )
 
-        def add(j):
-            def planes_0_1(d):
-                first = d * V + BAG[j]
-                apart = LAST_AT[j, d] - first
-                both = late[:, first : first + 2 * apart].rearrange("p (e s) -> p e s", e=2)[:, :, :P]
-                return both.rearrange("p e (c i) -> p c e i", i=2)
-
-            nc.vector.tensor_tensor(
-                x_bf[j].rearrange("p (c i t) -> p c t i", i=2, t=PACK)[:, :, 0:2, :],
-                planes_0_1(0),
-                planes_0_1(1),
-                ALU.add,
-            )
-
         def quantize(j):
             nc.vector.quantize_mx(
-                out=x_codes[j], scales=x_scales[:, j * P : (j + 1) * P], in_=x_bf[j]
-            )
-
-        def cast_w(m):
-            nc.scalar.activation(
-                out=w_bf[:, m * P * PACK : (m + 1) * P * PACK].rearrange("p (c i t) -> p c t i", i=4, t=PACK),
-                in_=w_raw[:, :, m * P : (m + 1) * P].rearrange("p t (c i) -> p c t i", i=4),
-                func=ACT.Copy,
+                out=x_words[:, j * P : (j + 1) * P].bitcast(FP8X4), scales=x_scales[:, j * P : (j + 1) * P], in_=x_bf[j]
             )
 
         def quantize_w(m):
             nc.vector.quantize_mx(
                 out=w_codes[:, m * P : (m + 1) * P].bitcast(FP8X4),
                 scales=w_scales[:, m * P : (m + 1) * P],
-                in_=w_bf[:, m * P * PACK : (m + 1) * P * PACK],
+                in_=w_bf[m],
             )
 
-        for d in range(D):
-            gather(last_pe[:, d * 2 * P : (d + 1) * 2 * P], 1, d * V + BAG[0], 2 * P)
-            for j in range(2):
-                piece = last_pe[:, (2 * d + j) * P : (2 * d + j + 1) * P]
-                nc.tensor.matmul(
-                    low_sums[j][:, 1, :], piece, ident[:], start=(d == 0), stop=(d == D - 1), is_transpose=True
-                )
         cast_w(0)
         cast_w(1)
-        low_pairs(0)
-        low_pairs(1)
         interleave(0)
         interleave(1)
-
-        def gather_last(j, d):
-            gather(late[:, LAST_AT[j, d] : LAST_AT[j, d] + P], 1, d * V + BAG[j], P)
-
-        gather(late[:, LAST_AT[2, 0] : LAST_AT[2, 0] + 2 * P], 1, BAG[2], 2 * P)
-        gather_last(2, 1)
-        gather_last(3, 1)
-        add(2)
-        add(3)
-        quantize_w(0)
         quantize(2)
+        quantize_w(0)
+        add(PACK - 1, 1)
         quantize_w(1)
         quantize(3)
         quantize(0)
@@ -250,7 +211,7 @@ def tile_picked_bag_lin_relu_sub_l_kernel(tc, xT, w, b, gate, offs, out):
                 out=acc,
                 lhsT=w_codes[:, m * P : (m + 1) * P].bitcast(FP8X4),
                 lhsT_scale=w_scales[:, m * P : (m + 1) * P],
-                rhs=x_codes[j],
+                rhs=x_words[:, j * P : (j + 1) * P].bitcast(FP8X4),
                 rhs_scale=x_scales[:, j * P : (j + 1) * P],
                 start=True,
                 stop=True,
@@ -263,16 +224,16 @@ def tile_picked_bag_lin_relu_sub_l_kernel(tc, xT, w, b, gate, offs, out):
             nc.vector.tensor_scalar(result[:, m, cols], acc, bias[:, m : m + 1], 0.0, ALU.add, ALU.max)
 
         relus = (relu_scalar, relu_vector)
-        accs = [psum.tile([P, 2 * P], F32, name="acc", tag="bank%d" % bank) for bank in (0, 6)]
+        accs = [psum.tile([P, H], F32, name="acc", tag="bank%d" % (6 + m)) for m in range(2)]
         for m, i in ((0, 0), (1, 0), (1, 1), (0, 1)):
-            product(accs[m][:, i * P : (i + 1) * P], m, 2 + i)
+            product(accs[1 - m][:, i * P : (i + 1) * P], m, 2 + i)
         for m in range(2):
-            relus[m](accs[m][:], m, slice(0, 2 * P))
-            nc.sync.dma_start(out=out[m * P : (m + 1) * P, : 2 * P], in_=result[:, m, : 2 * P])
-        for j, banks in ((0, (2, 3)), (1, (1, 5))):
-            for m in (j, 1 - j):
-                acc = psum.tile([P, P], F32, name="acc", tag="bank%d" % banks[m])
+            relus[m](accs[1 - m][:], m, slice(H, V))
+            nc.sync.dma_start(out=out[m * P : (m + 1) * P, H:], in_=result[:, m, H:])
+        for j in range(2):
+            for m in (1 - j, j):
+                acc = psum.tile([P, P], F32, name="acc", tag="bank%d" % (2 + 2 * j + m))
                 product(acc[:], m, j)
-                relus[m](acc[:], m, slice(BAG[j], BAG[j] + P))
+                relus[m](acc[:], m, slice(j * P, (j + 1) * P))
         for m in range(2):
-            nc.sync.dma_start(out=out[m * P : (m + 1) * P, 2 * P :], in_=result[:, m, 2 * P :])
+            nc.sync.dma_start(out=out[m * P : (m + 1) * P, :H], in_=result[:, m, :H])

@@ -40,10 +40,10 @@ def tile_picked_bag_lin_relu_sub_l_kernel(tc, xT, w, b, gate, offs, out):
         work = keep.tile([P, PICKS + 6 * H], F32, name="work", align_bytes=64)
         turned_b = keep.tile([P, 2, 2 * P], BF16, name="turned_b")
         x_picked = [keep.tile([P, P * PACK], BF16, name="x_picked%d" % j, align_bytes=64) for j in range(2)]
-        x_added = keep.tile([P, 2 * P * PACK + 16], BF16, name="x_added", align_bytes=64)
+        x_added = keep.tile([P, 32 + 2 * P * PACK], BF16, name="x_added", align_bytes=64)
         w_raw = keep.tile([P, PACK, N], F32, name="w_raw")
         w_bf = [work[:, at : at + H].bitcast(BF16) for at in (PICKS + PACK * H + P, PICKS + PACK * H - P)]
-        low_scaled = keep.tile([P, D * H], F32, name="low_scaled", tag="late", align_bytes=64)
+        low_scaled = [keep.tile([P, H], F32, name="low_scaled", tag=tag, align_bytes=64) for tag in ("late", "late_b")]
         w_codes = keep.tile([P, N], U32, name="w_codes", align_bytes=64)
         x_scales = keep.tile([P, V], U8, name="x_scales", align_bytes=64)
         w_scales = keep.tile([P, N], U8, name="w_scales", align_bytes=64)
@@ -71,7 +71,7 @@ def tile_picked_bag_lin_relu_sub_l_kernel(tc, xT, w, b, gate, offs, out):
 
         def scaled(u, j):
             if u == 0:
-                return low_scaled[:, j * H : (j + 1) * H].rearrange("v (e s) -> v e s", e=2)
+                return low_scaled[j][:].rearrange("v (e s) -> v e s", e=2)
             at = (2 + j) * STEP + H - P // 2
             return work[:, at : at + H].rearrange("v (e s) -> v e s", e=2)
 
@@ -96,7 +96,7 @@ def tile_picked_bag_lin_relu_sub_l_kernel(tc, xT, w, b, gate, offs, out):
             for j in range(2):
                 at = d * H + j * P
                 nc.tensor.transpose(gate_turned[d][:, j if d == 0 else 1 - j, :], gate_rows[:, at : at + P], ident_bf[:])
-        gate0 = x_added[:].bitcast(F32)[:, 2 * P : 4 * P + 1 : 2 * P]
+        gate0 = x_added[:].bitcast(F32)[:, 0 : 16 + 2 * P + 1 : 16 + 2 * P]
         at = PICKS + 2 * H
         gate1 = work[:, at : at + 3 * H : P].rearrange("p (n j) -> p n j", n=3)
         nc.vector.tensor_copy(out=gate1, in_=gate_turned[1][:, :, 0].unsqueeze(1).to_broadcast([P, 3, 2]))
@@ -114,7 +114,7 @@ def tile_picked_bag_lin_relu_sub_l_kernel(tc, xT, w, b, gate, offs, out):
                 return pair.rearrange("p e (c i) -> p c e i", i=2)
 
             t = PLANES[n - 1]
-            dst = x_added[:, j * P * PACK : (j + count) * P * PACK].rearrange("p (c i t) -> p c t i", i=2, t=PACK)
+            dst = x_added[:, 32 + j * P * PACK : 32 + (j + count) * P * PACK].rearrange("p (c i t) -> p c t i", i=2, t=PACK)
             nc.vector.tensor_tensor(dst[:, :, t : t + 2, :], both(0), both(1), ALU.add)
 
         for n, t in enumerate(PLANES):
@@ -168,7 +168,7 @@ def tile_picked_bag_lin_relu_sub_l_kernel(tc, xT, w, b, gate, offs, out):
                     nc.tensor.transpose(words[j][:, u, :], turned[j][u].bitcast(F32), ident[:])
 
         x_words = keep.tile([P, V], U32, name="x_words", tag="late", align_bytes=64)
-        x_bf = [x_picked[0][:], x_picked[1][:], x_added[:, : P * PACK], x_added[:, P * PACK : 2 * P * PACK]]
+        x_bf = [x_picked[0][:], x_picked[1][:], x_added[:, 32 : 32 + P * PACK], x_added[:, 32 + P * PACK :]]
 
         def cast_w(m):
             nc.scalar.activation(
@@ -224,16 +224,16 @@ def tile_picked_bag_lin_relu_sub_l_kernel(tc, xT, w, b, gate, offs, out):
             nc.vector.tensor_scalar(result[:, m, cols], acc, bias[:, m : m + 1], 0.0, ALU.add, ALU.max)
 
         relus = (relu_scalar, relu_vector)
-        accs = [psum.tile([P, H], F32, name="acc", tag="bank%d" % (6 + m)) for m in range(2)]
+        accs = [psum.tile([P, H], F32, name="acc", tag="bank%d" % m) for m in range(2)]
         for m, i in ((0, 0), (1, 0), (1, 1), (0, 1)):
-            product(accs[1 - m][:, i * P : (i + 1) * P], m, 2 + i)
-        for m in range(2):
-            relus[m](accs[1 - m][:], m, slice(H, V))
+            product(accs[m][:, i * P : (i + 1) * P], m, 2 + i)
+        for m in (1, 0):
+            relu_scalar(accs[m][:], m, slice(H, V))
             nc.sync.dma_start(out=out[m * P : (m + 1) * P, H:], in_=result[:, m, H:])
+        out_rows = out.rearrange("(m p) c -> p m c", p=P)
         for j in range(2):
-            for m in (1 - j, j):
+            for m in (j, 1 - j):
                 acc = psum.tile([P, P], F32, name="acc", tag="bank%d" % (2 + 2 * j + m))
                 product(acc[:], m, j)
                 relus[m](acc[:], m, slice(j * P, (j + 1) * P))
-        for m in range(2):
-            nc.sync.dma_start(out=out[m * P : (m + 1) * P, :H], in_=result[:, m, :H])
+            nc.sync.dma_start(out=out_rows[:, :, j * P : (j + 1) * P], in_=result[:, :, j * P : (j + 1) * P])

@@ -66,6 +66,8 @@ def tile_picked_bag_lin_relu_sub_l_kernel(tc, xT, w, b, gate, offs, out):
             return STEP + P if n == 0 else PICKS + n * H
 
         def picks(n, d, j):
+            if n == PACK - 1 and j == 1:
+                n, d, j = n - 1, 0, d
             at = picks_at(n) + (2 * d + j) * P // 2
             return work[:, at : at + P // 2].bitcast(BF16)
 
@@ -122,18 +124,21 @@ def tile_picked_bag_lin_relu_sub_l_kernel(tc, xT, w, b, gate, offs, out):
             if e == 0:
                 flipped = {}
                 for d in range(D):
-                    if u == 1 or d == 1:
+                    if u == 1:
                         both_tiles = psum.tile([P, 2, 2, P], BF16, name="flipped", tag="bank%d" % (2 + d))
                     for j in range(2):
-                        if u == 1 or d == 1:
+                        if u == 1:
                             flipped[j, d] = both_tiles[:, j]
                         else:
                             one = psum.tile([P, 2, P], BF16, name="flipped", tag="bank%d" % (2 + 2 * j + d))
                             flipped[j, d] = one[:]
             for d in (1, 0):
                 at = picks_at(n) + d * P
-                nc.scalar.activation(out=work[:, at : at + P].bitcast(BF16), in_=window(t, d * V, H), func=ACT.Copy)
+                if n < PACK - 1:
+                    nc.scalar.activation(out=work[:, at : at + P].bitcast(BF16), in_=window(t, d * V, H), func=ACT.Copy)
                 for j in range(2):
+                    if n == PACK - 1:
+                        nc.scalar.activation(out=picks(n, d, j), in_=window(t, d * V + j * P, P), func=ACT.Copy)
                     nc.tensor.transpose(flipped[j, d][:, e, :], picks(n, d, j), ident_bf[:])
             for d, first, count in ((0, 0, H), (1, 0, P), (1, P, P)) if n == PACK - 1 else ((0, 0, H), (1, 0, H)):
                 nc.vector.tensor_tensor(
@@ -230,10 +235,10 @@ def tile_picked_bag_lin_relu_sub_l_kernel(tc, xT, w, b, gate, offs, out):
         for m in (1, 0):
             relu_scalar(accs[m][:], m, slice(H, V))
             nc.sync.dma_start(out=out[m * P : (m + 1) * P, H:], in_=result[:, m, H:])
-        out_rows = out.rearrange("(m p) c -> p m c", p=P)
         for j in range(2):
             for m in (j, 1 - j):
                 acc = psum.tile([P, P], F32, name="acc", tag="bank%d" % (2 + 2 * j + m))
                 product(acc[:], m, j)
                 relus[m](acc[:], m, slice(j * P, (j + 1) * P))
-            nc.sync.dma_start(out=out_rows[:, :, j * P : (j + 1) * P], in_=result[:, :, j * P : (j + 1) * P])
+        for m in range(2):
+            nc.sync.dma_start(out=out[m * P : (m + 1) * P, :H], in_=result[:, m, :H])

@@ -40,7 +40,7 @@ def tile_picked_bag_lin_relu_sub_l_kernel(tc, xT, w, b, gate, offs, out):
         work = keep.tile([P, PICKS + 6 * H], F32, name="work", align_bytes=64)
         turned_b = keep.tile([P, 2, 2 * P], BF16, name="turned_b")
         x_picked = [keep.tile([P, P * PACK], BF16, name="x_picked%d" % j, align_bytes=64) for j in range(2)]
-        x_added = keep.tile([P, 32 + 2 * P * PACK], BF16, name="x_added", align_bytes=64)
+        x_added = keep.tile([P, 2 * P * PACK + 16], BF16, name="x_added", align_bytes=64)
         w_raw = keep.tile([P, PACK, N], F32, name="w_raw")
         w_bf = [work[:, at : at + H].bitcast(BF16) for at in (PICKS + PACK * H + P, PICKS + PACK * H - P)]
         low_scaled = [keep.tile([P, H], F32, name="low_scaled", tag=tag, align_bytes=64) for tag in ("late", "late_b")]
@@ -98,7 +98,7 @@ def tile_picked_bag_lin_relu_sub_l_kernel(tc, xT, w, b, gate, offs, out):
             for j in range(2):
                 at = d * H + j * P
                 nc.tensor.transpose(gate_turned[d][:, j if d == 0 else 1 - j, :], gate_rows[:, at : at + P], ident_bf[:])
-        gate0 = x_added[:].bitcast(F32)[:, 0 : 16 + 2 * P + 1 : 16 + 2 * P]
+        gate0 = x_added[:].bitcast(F32)[:, 2 * P : 4 * P + 1 : 2 * P]
         at = PICKS + 2 * H
         gate1 = work[:, at : at + 3 * H : P].rearrange("p (n j) -> p n j", n=3)
         nc.vector.tensor_copy(out=gate1, in_=gate_turned[1][:, :, 0].unsqueeze(1).to_broadcast([P, 3, 2]))
@@ -116,7 +116,7 @@ def tile_picked_bag_lin_relu_sub_l_kernel(tc, xT, w, b, gate, offs, out):
                 return pair.rearrange("p e (c i) -> p c e i", i=2)
 
             t = PLANES[n - 1]
-            dst = x_added[:, 32 + j * P * PACK : 32 + (j + count) * P * PACK].rearrange("p (c i t) -> p c t i", i=2, t=PACK)
+            dst = x_added[:, j * P * PACK : (j + count) * P * PACK].rearrange("p (c i t) -> p c t i", i=2, t=PACK)
             nc.vector.tensor_tensor(dst[:, :, t : t + 2, :], both(0), both(1), ALU.add)
 
         for n, t in enumerate(PLANES):
@@ -172,8 +172,10 @@ def tile_picked_bag_lin_relu_sub_l_kernel(tc, xT, w, b, gate, offs, out):
                     )
                     nc.tensor.transpose(words[j][:, u, :], turned[j][u].bitcast(F32), ident[:])
 
+        add(PACK - 1, 1)
+
         x_words = keep.tile([P, V], U32, name="x_words", tag="late", align_bytes=64)
-        x_bf = [x_picked[0][:], x_picked[1][:], x_added[:, 32 : 32 + P * PACK], x_added[:, 32 + P * PACK :]]
+        x_bf = [x_picked[0][:], x_picked[1][:], x_added[:, : P * PACK], x_added[:, P * PACK : 2 * P * PACK]]
 
         def cast_w(m):
             nc.scalar.activation(
@@ -205,9 +207,8 @@ def tile_picked_bag_lin_relu_sub_l_kernel(tc, xT, w, b, gate, offs, out):
         interleave(1)
         quantize(2)
         quantize_w(0)
-        add(PACK - 1, 1)
-        quantize_w(1)
         quantize(3)
+        quantize_w(1)
         quantize(0)
         quantize(1)
 
@@ -230,15 +231,15 @@ def tile_picked_bag_lin_relu_sub_l_kernel(tc, xT, w, b, gate, offs, out):
 
         relus = (relu_scalar, relu_vector)
         accs = [psum.tile([P, H], F32, name="acc", tag="bank%d" % m) for m in range(2)]
-        for m, i in ((0, 0), (1, 0), (1, 1), (0, 1)):
+        for m, i in ((0, 0), (0, 1), (1, 1), (1, 0)):
             product(accs[m][:, i * P : (i + 1) * P], m, 2 + i)
-        for m in (1, 0):
+        for m in range(2):
             relu_scalar(accs[m][:], m, slice(H, V))
             nc.sync.dma_start(out=out[m * P : (m + 1) * P, H:], in_=result[:, m, H:])
         for j in range(2):
-            for m in (j, 1 - j):
+            for m in (1 - j, j):
                 acc = psum.tile([P, P], F32, name="acc", tag="bank%d" % (2 + 2 * j + m))
                 product(acc[:], m, j)
-                relus[m](acc[:], m, slice(j * P, (j + 1) * P))
+                relus[m if j else 1](acc[:], m, slice(j * P, (j + 1) * P))
         for m in range(2):
             nc.sync.dma_start(out=out[m * P : (m + 1) * P, :H], in_=result[:, m, :H])

@@ -98,7 +98,7 @@ def tile_picked_bag_lin_relu_sub_l_kernel(tc, xT, w, b, gate, offs, out):
             for j in range(2):
                 at = d * H + j * P
                 nc.tensor.transpose(gate_turned[d][:, j if d == 0 else 1 - j, :], gate_rows[:, at : at + P], ident_bf[:])
-        gate0 = x_added[:].bitcast(F32)[:, 2 * P : 4 * P + 1 : 2 * P]
+        gate0 = x_added[:].bitcast(F32)[:, 4 * P : 4 * P + 2]
         at = PICKS + 2 * H
         gate1 = work[:, at : at + 3 * H : P].rearrange("p (n j) -> p n j", n=3)
         nc.vector.tensor_copy(out=gate1, in_=gate_turned[1][:, :, 0].unsqueeze(1).to_broadcast([P, 3, 2]))
@@ -109,7 +109,7 @@ def tile_picked_bag_lin_relu_sub_l_kernel(tc, xT, w, b, gate, offs, out):
         def window(t, e0, count):
             return planes[t][:].indirect(offsets[:, e0 // 16 : (e0 + count) // 16])
 
-        def add(n, j, count=1):
+        def add(n, j, count=1, engine=nc.vector):
             def both(d):
                 at = (n - 1) * STEP + d * H + j * P
                 pair = work[:, at : at + 2 * STEP].rearrange("p (e s) -> p e s", e=2)[:, :, : count * P]
@@ -117,7 +117,7 @@ def tile_picked_bag_lin_relu_sub_l_kernel(tc, xT, w, b, gate, offs, out):
 
             t = PLANES[n - 1]
             dst = x_added[:, j * P * PACK : (j + count) * P * PACK].rearrange("p (c i t) -> p c t i", i=2, t=PACK)
-            nc.vector.tensor_tensor(dst[:, :, t : t + 2, :], both(0), both(1), ALU.add)
+            engine.tensor_tensor(dst[:, :, t : t + 2, :], both(0), both(1), ALU.add)
 
         for n, t in enumerate(PLANES):
             u, e = t // 2, t % 2
@@ -172,7 +172,7 @@ def tile_picked_bag_lin_relu_sub_l_kernel(tc, xT, w, b, gate, offs, out):
                     )
                     nc.tensor.transpose(words[j][:, u, :], turned[j][u].bitcast(F32), ident[:])
 
-        add(PACK - 1, 1)
+        add(PACK - 1, 1, engine=nc.gpsimd)
 
         x_words = keep.tile([P, V], U32, name="x_words", tag="late", align_bytes=64)
         x_bf = [x_picked[0][:], x_picked[1][:], x_added[:, : P * PACK], x_added[:, P * PACK : 2 * P * PACK]]

@@ -31,8 +31,8 @@ def tile_picked_bag_lin_relu_sub_l_kernel(tc, xT, w, b, gate, offs, out):
 
         offsets = keep.tile([P, D * V // 16], U16, name="offsets")
         planes = [keep.tile([P, T], F32, name="plane%d" % t) for t in range(PACK)]
-        gate_cols = keep.tile([P, D, 2 * PACK], F32, name="gate_cols")
-        gate_bf = keep.tile([P, D, PACK], BF16, name="gate_bf")
+        gate_cols = keep.tile([P, D * PACK], F32, name="gate_cols")
+        gate_bf = keep.tile([P, D * PACK], BF16, name="gate_bf")
         gates = keep.tile([P, D * H], F32, name="gates")
         ident_bf = keep.tile([P, P], BF16, name="ident_bf")
         ident = keep.tile([P, P], F32, name="ident")
@@ -50,7 +50,8 @@ def tile_picked_bag_lin_relu_sub_l_kernel(tc, xT, w, b, gate, offs, out):
         result = keep.tile([P, N // P, V], F32, name="result")
 
         x_rows = xT.rearrange("(p t) c -> p t c", t=PACK)
-        nc.sync.dma_start(out=gate_cols[:, :, :PACK], in_=gate[:, 0, :].rearrange("d (p j) -> p d j", j=PACK))
+        gate_runs = gate.rearrange("d r (a j) -> (d r a) j", j=D * PACK)
+        nc.sync.dma_start(out=gate_cols[:], in_=gate_runs[:: P + 1, :])
         nc.sync.dma_start(out=planes[PLANES[0]][:], in_=x_rows[:, PLANES[0], :])
         nc.sync.dma_start(offsets[:], offs)
         for t in PLANES[1:]:
@@ -84,15 +85,14 @@ def tile_picked_bag_lin_relu_sub_l_kernel(tc, xT, w, b, gate, offs, out):
         ]
         make_identity(nc, ident[:])
         make_identity(nc, ident_bf[:])
-        nc.scalar.activation(out=gate_bf[:], in_=gate_cols[:, :, :PACK], func=ACT.Copy)
-        spread = psum.tile([P, D, 2, P], F32, name="spread", tag="bank0")
-        for d in range(D):
-            for u in range(2):
-                word = gate_bf[:, d, :].bitcast(F32)[:, u : u + 1]
-                nc.tensor.transpose(spread[:, d, u, :], word.to_broadcast([P, P]), ident[:])
-        by_bag = spread[:].bitcast(BF16).rearrange("m d u (p e) -> m d p u e", e=2)
-        for dst, half in ((gate_rows, by_bag[:, :, : P // 2]), (gates[:], by_bag[:, :, P // 2 :])):
-            nc.vector.tensor_copy(out=dst.rearrange("m (d p u e) -> m d p u e", d=D, u=2, e=2), in_=half)
+        nc.scalar.activation(out=gate_bf[:], in_=gate_cols[:], func=ACT.Copy)
+        spread = psum.tile([P, PACK, P], F32, name="spread", tag="bank0")
+        for u in range(PACK):
+            word = gate_bf[:].bitcast(F32)[:, u : u + 1]
+            nc.tensor.transpose(spread[:, u, :], word.to_broadcast([P, P]), ident[:])
+        by_bag = spread[:].bitcast(BF16).rearrange("m u (d h q e) -> m h d q u e", d=D, h=2, e=2)
+        for half, dst in enumerate((gate_rows, gates[:])):
+            nc.vector.tensor_copy(out=dst.rearrange("m (d q u e) -> m d q u e", d=D, u=PACK, e=2), in_=by_bag[:, half])
         gate_turned = [psum.tile([P, 2, P], BF16, name="gate_turned", tag="bank%d" % (2 + d)) for d in range(D)]
         for d in (1, 0):
             for j in range(2):
@@ -230,12 +230,16 @@ def tile_picked_bag_lin_relu_sub_l_kernel(tc, xT, w, b, gate, offs, out):
             nc.vector.tensor_scalar(result[:, m, cols], acc, bias[:, m : m + 1], 0.0, ALU.add, ALU.max)
 
         relus = (relu_scalar, relu_vector)
-        accs = [psum.tile([P, H], F32, name="acc", tag="bank%d" % m) for m in range(2)]
-        for m, i in ((0, 0), (0, 1), (1, 1), (1, 0)):
-            product(accs[m][:, i * P : (i + 1) * P], m, 2 + i)
-        for m in range(2):
-            relu_scalar(accs[m][:], m, slice(H, V))
-            nc.sync.dma_start(out=out[m * P : (m + 1) * P, H:], in_=result[:, m, H:])
+        acc = psum.tile([P, H], F32, name="acc", tag="bank0")
+        for i in range(2):
+            product(acc[:, i * P : (i + 1) * P], 0, 2 + i)
+        relu_scalar(acc[:], 0, slice(H, V))
+        nc.sync.dma_start(out=out[:P, H:], in_=result[:, 0, H:])
+        for i, bank in ((1, 1), (0, 6)):
+            acc = psum.tile([P, P], F32, name="acc", tag="bank%d" % bank)
+            product(acc[:], 1, 2 + i)
+            relu_scalar(acc[:], 1, slice(H + i * P, H + (i + 1) * P))
+        nc.sync.dma_start(out=out[P:, H:], in_=result[:, 1, H:])
         for j in range(2):
             for m in (1 - j, j):
                 acc = psum.tile([P, P], F32, name="acc", tag="bank%d" % (2 + 2 * j + m))

@@ -149,7 +149,7 @@ def tile_picked_bag_lin_relu_sub_l_kernel(tc, xT, w, b, gate, offs, out):
                 )
             if n == 1:
                 add(n, 0)
-                add(n, 1)
+                add(n, 1, engine=nc.gpsimd)
             if n == PACK - 1:
                 add(n, 0)
             for j in range(2):

from contextlib import ExitStack

import concourse.mybir as mybir
from concourse.masks import make_identity

K, T, D, V, N = 512, 2048, 2, 512, 256
FLOPS = 2 * K * N * V

F32 = mybir.dt.float32
BF16 = mybir.dt.bfloat16
U32 = mybir.dt.uint32
U16 = mybir.dt.uint16
U8 = mybir.dt.uint8
FP8X4 = mybir.dt.float8_e4m3fn_x4
ALU = mybir.AluOpType
ACT = mybir.ActivationFunctionType

P = 128
PACK = 4
H = V // 2
PLANES = (2, 3, 0, 1)
STEP = D * H
PICKS = PACK * STEP


def tile_picked_bag_lin_relu_sub_l_kernel(tc, xT, w, b, gate, offs, out):
    nc = tc.nc
    with ExitStack() as ctx:
        keep = ctx.enter_context(tc.tile_pool(name="keep", bufs=1))
        psum = ctx.enter_context(tc.psum_pool(name="psum", bufs=1))

        offsets = keep.tile([P, D * V // 16], U16, name="offsets")
        planes = [keep.tile([P, T], F32, name="plane%d" % t) for t in range(PACK)]
        gate_cols = keep.tile([P, D * PACK], F32, name="gate_cols")
        gate_bf = keep.tile([P, D * PACK], BF16, name="gate_bf")
        gates = keep.tile([P, D * H], F32, name="gates")
        ident_bf = keep.tile([P, P], BF16, name="ident_bf")
        ident = keep.tile([P, P], F32, name="ident")
        bias = keep.tile([P, N // P], F32, name="bias")
        work = keep.tile([P, PICKS + 6 * H], F32, name="work", align_bytes=64)
        turned_b = keep.tile([P, 2, 2 * P], BF16, name="turned_b")
        x_picked = [keep.tile([P, P * PACK], BF16, name="x_picked%d" % j, align_bytes=64) for j in range(2)]
        x_added = keep.tile([P, 2 * P * PACK + 16], BF16, name="x_added", align_bytes=64)
        w_raw = keep.tile([P, PACK, N], F32, name="w_raw")
        w_bf = [work[:, at : at + H].bitcast(BF16) for at in (PICKS + PACK * H + P, PICKS + PACK * H - P)]
        low_scaled = [keep.tile([P, H], F32, name="low_scaled", tag=tag, align_bytes=64) for tag in ("late", "late_b")]
        w_codes = keep.tile([P, N], U32, name="w_codes", align_bytes=64)
        x_scales = keep.tile([P, V], U8, name="x_scales", align_bytes=64)
        w_scales = keep.tile([P, N], U8, name="w_scales", align_bytes=64)
        result = keep.tile([P, N // P, V], F32, name="result")

        x_rows = xT.rearrange("(p t) c -> p t c", t=PACK)
        gate_runs = gate.rearrange("d r (a j) -> (d r a) j", j=D * PACK)
        nc.sync.dma_start(out=gate_cols[:], in_=gate_runs[:: P + 1, :])
        nc.sync.dma_start(out=planes[PLANES[0]][:], in_=x_rows[:, PLANES[0], :])
        nc.sync.dma_start(offsets[:], offs)
        for t in PLANES[1:]:
            nc.sync.dma_start(out=planes[t][:], in_=x_rows[:, t, :])
        nc.sync.dma_start(out=w_raw[:], in_=w.rearrange("(p t) c -> p t c", t=PACK))
        with nc.allow_non_contiguous_dma(reason="one bias value to a partition"):
            nc.sync.dma_start(out=bias[:], in_=b.rearrange("(c p) o -> p (c o)", p=P))

        def products(n, d):
            return work[:, n * STEP + d * H : n * STEP + (d + 1) * H]

        def picks_at(n):
            return STEP + P if n == 0 else PICKS + n * H

        def picks(n, d, j):
            if n == PACK - 1 and j == 1:
                n, d, j = n - 1, 0, d
            at = picks_at(n) + (2 * d + j) * P // 2
            return work[:, at : at + P // 2].bitcast(BF16)

        def scaled(u, j):
            if u == 0:
                return low_scaled[j][:].rearrange("v (e s) -> v e s", e=2)
            at = (2 + j) * STEP + H - P // 2
            return work[:, at : at + H].rearrange("v (e s) -> v e s", e=2)

        gate_rows = work[:, PICKS : PICKS + H].bitcast(BF16)
        turned = [
            [gates[:, 3 * P :].bitcast(BF16), work[:, :P].bitcast(BF16)],
            [turned_b[:, 0, :], turned_b[:, 1, :]],
        ]
        make_identity(nc, ident[:])
        make_identity(nc, ident_bf[:])
        nc.scalar.activation(out=gate_bf[:], in_=gate_cols[:], func=ACT.Copy)
        spread = psum.tile([P, PACK, P], F32, name="spread", tag="bank0")
        for u in range(PACK):
            word = gate_bf[:].bitcast(F32)[:, u : u + 1]
            nc.tensor.transpose(spread[:, u, :], word.to_broadcast([P, P]), ident[:])
        by_bag = spread[:].bitcast(BF16).rearrange("m u (d h q e) -> m h d q u e", d=D, h=2, e=2)
        for half, dst in enumerate((gate_rows, gates[:])):
            nc.vector.tensor_copy(out=dst.rearrange("m (d q u e) -> m d q u e", d=D, u=PACK, e=2), in_=by_bag[:, half])
        gate_turned = [psum.tile([P, 2, P], BF16, name="gate_turned", tag="bank%d" % (2 + d)) for d in range(D)]
        for d in (1, 0):
            for j in range(2):
                at = d * H + j * P
                nc.tensor.transpose(gate_turned[d][:, j if d == 0 else 1 - j, :], gate_rows[:, at : at + P], ident_bf[:])
        gate0 = x_added[:].bitcast(F32)[:, 4 * P : 4 * P + 2]
        at = PICKS + 2 * H
        gate1 = work[:, at : at + 3 * H : P].rearrange("p (n j) -> p n j", n=3)
        nc.vector.tensor_copy(out=gate1, in_=gate_turned[1][:, :, 0].unsqueeze(1).to_broadcast([P, 3, 2]))
        nc.vector.tensor_copy(out=gate0, in_=gate_turned[0][:, :, 0])

        words = [psum.tile([P, 2, P], F32, name="words", tag="bank%d" % (6 + j)) for j in range(2)]

        def window(t, e0, count):
            return planes[t][:].indirect(offsets[:, e0 // 16 : (e0 + count) // 16])

        def add(n, j, count=1, engine=nc.vector):
            def both(d):
                at = (n - 1) * STEP + d * H + j * P
                pair = work[:, at : at + 2 * STEP].rearrange("p (e s) -> p e s", e=2)[:, :, : count * P]
                return pair.rearrange("p e (c i) -> p c e i", i=2)

            t = PLANES[n - 1]
            dst = x_added[:, j * P * PACK : (j + count) * P * PACK].rearrange("p (c i t) -> p c t i", i=2, t=PACK)
            engine.tensor_tensor(dst[:, :, t : t + 2, :], both(0), both(1), ALU.add)

        for n, t in enumerate(PLANES):
            u, e = t // 2, t % 2
            if e == 0:
                flipped = {}
                for d in range(D):
                    if u == 1:
                        both_tiles = psum.tile([P, 2, 2, P], BF16, name="flipped", tag="bank%d" % (2 + d))
                    for j in range(2):
                        if u == 1:
                            flipped[j, d] = both_tiles[:, j]
                        else:
                            one = psum.tile([P, 2, P], BF16, name="flipped", tag="bank%d" % (2 + 2 * j + d))
                            flipped[j, d] = one[:]
            for d in (1, 0):
                at = picks_at(n) + d * P
                if n < PACK - 1:
                    nc.scalar.activation(out=work[:, at : at + P].bitcast(BF16), in_=window(t, d * V, H), func=ACT.Copy)
                for j in range(2):
                    if n == PACK - 1:
                        nc.scalar.activation(out=picks(n, d, j), in_=window(t, d * V + j * P, P), func=ACT.Copy)
                    nc.tensor.transpose(flipped[j, d][:, e, :], picks(n, d, j), ident_bf[:])
            for d, first, count in ((0, 0, H), (1, 0, P), (1, P, P)) if n == PACK - 1 else ((0, 0, H), (1, 0, H)):
                nc.vector.tensor_tensor(
                    products(n, d)[:, first : first + count],
                    window(t, d * V + H + first, count),
                    gates[:, d * H + first : d * H + first + count],
                    ALU.mult,
                )
            if n == 1:
                add(n, 0)
                add(n, 1, engine=nc.gpsimd)
            if n == PACK - 1:
                add(n, 0)
            for j in range(2):
                if n > 0:
                    part = slice(0, 2) if u == 1 else slice(e, e + 1)
                    nc.scalar.activation(
                        out=scaled(u, j)[:, part],
                        in_=flipped[j, 1][:, part],
                        func=ACT.Copy,
                        scale=gate1[:, n - 1, 1 - j : 2 - j],
                    )
                if e == 1:
                    nc.vector.scalar_tensor_tensor(
                        turned[j][u].rearrange("v (p e) -> v p e", e=2),
                        flipped[j, 0].rearrange("v e p -> v p e"),
                        gate0[:, j : j + 1],
                        scaled(u, j).rearrange("v e p -> v p e"),
                        ALU.mult,
                        ALU.add,
                    )
                    nc.tensor.transpose(words[j][:, u, :], turned[j][u].bitcast(F32), ident[:])

        add(PACK - 1, 1, engine=nc.gpsimd)

        x_words = keep.tile([P, V], U32, name="x_words", tag="late", align_bytes=64)
        x_bf = [x_picked[0][:], x_picked[1][:], x_added[:, : P * PACK], x_added[:, P * PACK : 2 * P * PACK]]

        def cast_w(m):
            nc.scalar.activation(
                out=w_bf[m].rearrange("p (c i t) -> p c t i", i=4, t=PACK),
                in_=w_raw[:, :, m * P : (m + 1) * P].rearrange("p t (c i) -> p c t i", i=4),
                func=ACT.Copy,
            )

        def interleave(j):
            nc.scalar.copy(
                out=x_bf[j].bitcast(F32).rearrange("p (v u) -> p v u", u=2), in_=words[j][:].rearrange("p u v -> p v u")
            )

        def quantize(j):
            nc.vector.quantize_mx(
                out=x_words[:, j * P : (j + 1) * P].bitcast(FP8X4), scales=x_scales[:, j * P : (j + 1) * P], in_=x_bf[j]
            )

        def quantize_w(m):
            nc.vector.quantize_mx(
                out=w_codes[:, m * P : (m + 1) * P].bitcast(FP8X4),
                scales=w_scales[:, m * P : (m + 1) * P],
                in_=w_bf[m],
            )

        cast_w(0)
        cast_w(1)
        interleave(0)
        interleave(1)
        quantize(2)
        quantize_w(0)
        quantize(3)
        quantize_w(1)
        quantize(0)
        quantize(1)

        def product(acc, m, j):
            nc.tensor.matmul_mx(
                out=acc,
                lhsT=w_codes[:, m * P : (m + 1) * P].bitcast(FP8X4),
                lhsT_scale=w_scales[:, m * P : (m + 1) * P],
                rhs=x_words[:, j * P : (j + 1) * P].bitcast(FP8X4),
                rhs_scale=x_scales[:, j * P : (j + 1) * P],
                start=True,
                stop=True,
            )

        def relu_scalar(acc, m, cols):
            nc.scalar.activation(out=result[:, m, cols], in_=acc, func=ACT.Relu, bias=bias[:, m : m + 1])

        def relu_vector(acc, m, cols):
            nc.vector.tensor_scalar(result[:, m, cols], acc, bias[:, m : m + 1], 0.0, ALU.add, ALU.max)

        relus = (relu_scalar, relu_vector)
        acc = psum.tile([P, H], F32, name="acc", tag="bank0")
        for i in range(2):
            product(acc[:, i * P : (i + 1) * P], 0, 2 + i)
        relu_scalar(acc[:], 0, slice(H, V))
        nc.sync.dma_start(out=out[:P, H:], in_=result[:, 0, H:])
        for i, bank in ((1, 1), (0, 6)):
            acc = psum.tile([P, P], F32, name="acc", tag="bank%d" % bank)
            product(acc[:], 1, 2 + i)
            relu_scalar(acc[:], 1, slice(H + i * P, H + (i + 1) * P))
        nc.sync.dma_start(out=out[P:, H:], in_=result[:, 1, H:])
        for j in range(2):
            for m in (1 - j, j):
                acc = psum.tile([P, P], F32, name="acc", tag="bank%d" % (2 + 2 * j + m))
                product(acc[:], m, j)
                relus[m if j else 1](acc[:], m, slice(j * P, (j + 1) * P))
        for m in range(2):
            nc.sync.dma_start(out=out[m * P : (m + 1) * P, :H], in_=result[:, m, :H])
